import numpy as np
import ml_dtypes


def mxq(x, axis, fmt="e4m3"):
    dtype, down = {"e4m3": (ml_dtypes.float8_e4m3fn, 7), "e5m2": (ml_dtypes.float8_e5m2, 14)}[fmt]
    v = np.moveaxis(np.asarray(x, np.float32).astype(ml_dtypes.bfloat16).astype(np.float64), axis, -1)
    blocks = v.reshape(v.shape[:-1] + (-1, 32))
    amax = np.abs(blocks).max(-1, keepdims=True)
    byte = np.maximum(np.where(amax > 0, np.frexp(amax)[1] - 1 + 127, 0) - down, 1)
    scale = np.exp2(byte - 127.0)
    codes = (blocks / scale).astype(np.float32).astype(dtype).astype(np.float64)
    return np.moveaxis((codes * scale).reshape(v.shape), -1, axis)


WIDE = False


def mx_kscale(k):
    if not WIDE:
        return np.ones(k)
    levels = np.array([10, -10, 5, -5, 0])
    if k % 512:
        return np.exp2(np.random.permutation(np.resize(levels, k // 32))).repeat(32)
    a = np.empty((k // 512, 16))
    for p in range(k // 512):
        a[p, :8] = np.random.permutation(np.resize(levels, 8))
        for g in range(8):
            far = levels[np.abs(levels - a[p, g]) >= 10]
            a[p, g + 8] = far[np.random.randint(len(far))]
    return np.exp2(a.ravel()).repeat(32)


def f64(x):
    return np.asarray(x).astype(np.float64)


def striped(idx):
    return np.tile(idx.reshape(-1, 16).T, (8, 1)).astype(np.uint16)


def unstriped(offs):
    return offs[:16].T.reshape(-1).astype(np.int64)


E2M1 = np.array([0.0, 0.5, 1.0, 1.5, 2.0, 3.0, 4.0, 6.0, -0.0, -0.5, -1.0, -1.5, -2.0, -3.0, -4.0, -6.0])


def pack_weight(w, fmt):
    k, n = w.shape
    w = f64(np.asarray(w, np.float32).astype(ml_dtypes.bfloat16)).reshape(k // 32, 32, n)
    amax = np.abs(w).max(1)
    if fmt == "e4m3":
        byte = np.frexp(amax)[1] - 1 + 127 - 7
    else:
        mant, ex = np.frexp(amax / 6.0)
        byte = np.where(mant > 0.5, ex, ex - 1) + 127
    byte = np.clip(np.where(amax > 0, byte, 1), 1, 254)
    scaled = (w * np.exp2(127.0 - byte)[:, None, :]).reshape(k, n).astype(np.float32)
    by_word = np.ascontiguousarray(scaled.reshape(k // 512, 128, 4, n).transpose(0, 1, 3, 2))
    if fmt == "e4m3":
        words = by_word.astype(ml_dtypes.float8_e4m3fn).view(np.uint8)
    else:
        c = by_word.astype(ml_dtypes.float4_e2m1fn).view(np.uint8) & 0xF
        words = (c[..., 0::2] | (c[..., 1::2] << 4)).reshape(k // 512, 128, 2 * n)
    return np.ascontiguousarray(words), np.ascontiguousarray(byte.astype(np.uint8).reshape(k // 512, 16, n))


def unpack_weight(words, scales, fmt):
    g, _, n = scales.shape
    words = np.ascontiguousarray(words).reshape(g, 128, n, -1)
    if fmt == "e4m3":
        vals = words.view(ml_dtypes.float8_e4m3fn).astype(np.float64)
    else:
        nib = np.empty((g, 128, n, 4), np.uint8)
        nib[..., 0::2] = words & 0xF
        nib[..., 1::2] = words >> 4
        vals = E2M1[nib]
    vals = vals * np.repeat(np.exp2(scales.astype(np.float64) - 127.0), 8, axis=1)[..., None]
    return vals.transpose(0, 1, 3, 2).reshape(g * 512, n)


def gelu(v):
    return 0.5 * v * (1.0 + np.tanh(np.sqrt(2.0 / np.pi) * (v + 0.044715 * v**3)))


def striped8(idx):
    return np.concatenate([v.reshape(-1, 16).T for v in idx]).astype(np.uint16)


def unstriped8(offs):
    return np.stack([offs[16 * g:16 * g + 16].T.reshape(-1) for g in range(8)]).astype(np.int64)


def heads(h, wgt, idx8):
    r = np.arange(h.shape[0])
    return wgt[r // 4 % 128] * h[r[:, None], idx8[r % 512 // 64]]


K, T, S, H, P, N = 1024, 4096, 2048, 1024, 1024, 384

def setup_inputs():
    n = np.random.standard_normal
    s = mx_kscale(K)[:, None]
    u = mx_kscale(H)[:, None]
    tab_words, tab_scales = pack_weight(n((K, T)) * s, "e4m3")
    offs = striped(np.random.permutation(T)[:S])
    w1 = (n((K, H)) / np.sqrt(K) / s * u.T).astype(np.float32)
    offs2 = striped8(np.stack([np.random.permutation(S)[:P] for _ in range(8)]))
    wgt = np.repeat(np.random.uniform(0.5, 2.0, (8, P)), 16, axis=0).astype(np.float32)
    w2_words, w2_scales = pack_weight(n((H, N)) / np.sqrt(H) / u, "e2m1")
    return {"tab_words": tab_words, "tab_scales": tab_scales, "offs": offs, "w1": w1,
            "offs2": offs2, "wgt": wgt, "w2_words": w2_words, "w2_scales": w2_scales}

def reference(tab_words, tab_scales, offs, w1, offs2, wgt, w2_words, w2_scales):
    v = unpack_weight(tab_words, tab_scales, "e4m3")[:, unstriped(offs)]
    w1q = mxq(f64(w1), 0, "e4m3")
    h = w1q.T @ v
    x = heads(h, f64(wgt), unstriped8(offs2))
    z = np.maximum(x, 0.0)
    zq = mxq(z, 0, "e4m3")
    w2 = unpack_weight(w2_words, w2_scales, "e2m1")
    out = w2.T @ zq
    return out

@@ -1,0 +1,191 @@
+from contextlib import ExitStack
+
+import concourse.mybir as mybir
+
+K, T, S, H, G, N = 1024, 4096, 2048, 1024, 1024, 384
+FLOPS = 2 * K * H * S + 2 * H * N * G
+
+F32 = mybir.dt.float32
+BF16 = mybir.dt.bfloat16
+I32 = mybir.dt.int32
+U32 = mybir.dt.uint32
+U16 = mybir.dt.uint16
+U8 = mybir.dt.uint8
+FP8X4 = mybir.dt.float8_e4m3fn_x4
+FP4X4 = mybir.dt.float4_e2m1fn_x4
+ALU = mybir.AluOpType
+ACT = mybir.ActivationFunctionType
+
+P = 128
+PACK = 4
+PASS = P * PACK
+COLS = 512
+
+
+def tile_list_premise_selection_kernel(tc, tab_words, tab_scales, offs, w1, offs2, wgt, w2_words, w2_scales, out):
+    nc = tc.nc
+    with ExitStack() as ctx:
+        lists = ctx.enter_context(tc.tile_pool(name="lists", bufs=1))
+        keep = ctx.enter_context(tc.tile_pool(name="keep", bufs=1))
+        psum = ctx.enter_context(tc.psum_pool(name="psum", bufs=8))
+
+        idx = lists.tile([P, S // 16], U16, name="idx")
+        idx2 = lists.tile([P, G // 16], U16, name="idx2")
+
+        table = [keep.tile([P, T], I32, name=f"table{a}", align_bytes=64) for a in range(2)]
+        table_sc = keep.tile([P, T], U8, name="table_sc", tag="sc_then_v0", align_bytes=64)
+        w2_sc = keep.tile([P, 2 * N], U8, name="w2_sc", align_bytes=64)
+        w2_wd = keep.tile([P, 2, 2 * N], U8, name="w2_wd", align_bytes=64)
+        wgt_sb = keep.tile([P, G], F32, name="wgt_sb", align_bytes=64)
+        w1_raw = {}
+        for b in range(2):
+            for a in range(2):
+                w1_raw[b, a] = keep.tile([P, PACK, PASS], F32, name=f"w1_raw{b}{a}", align_bytes=64)
+
+        nc.vector.memset(table_sc[:].bitcast(I32), 0)
+        nc.vector.memset(w2_sc[:].bitcast(I32), 0)
+
+        def load_w1(b, a):
+            rows = w1[a * PASS:(a + 1) * PASS, b * PASS:(b + 1) * PASS]
+            nc.sync.dma_start(out=w1_raw[b, a][:], in_=rows.rearrange("(p j) c -> p j c", j=PACK))
+
+        def load_table(a):
+            nc.sync.dma_start(out=table[a][:], in_=tab_words[a].rearrange("p t i -> p (t i)").bitcast(I32))
+
+        nc.sync.dma_start(idx[:], offs)
+        load_table(0)
+        for a in range(2):
+            for q in range(4):
+                nc.scalar.dma_start(out=table_sc[32 * q + 4 * a:32 * q + 4 * a + 4, :].bitcast(I32),
+                                    in_=tab_scales[a, 4 * q:4 * q + 4, :].bitcast(I32))
+        load_w1(0, 0)
+        load_w1(0, 1)
+        load_table(1)
+        nc.sync.dma_start(idx2[:], offs2)
+        nc.sync.dma_start(out=wgt_sb[:], in_=wgt)
+        load_w1(1, 0)
+        load_w1(1, 1)
+        nc.sync.dma_start(out=w2_wd[:].bitcast(I32), in_=w2_words.rearrange("a p c -> p a c").bitcast(I32))
+        for q in range(4):
+            nc.sync.dma_start(
+                out=w2_sc[32 * q:32 * q + 4, :].rearrange("r (a n) -> r a n", a=2).bitcast(I32),
+                in_=w2_scales[:, 4 * q:4 * q + 4, :].rearrange("a r n -> r a n").bitcast(I32))
+
+        v_sc = keep.tile([P, S], U8, name="v_sc", align_bytes=64)
+        v1 = [keep.tile([P, COLS], U32, name=f"v1_{c}", align_bytes=64) for c in range(S // COLS)]
+
+        w1_q = {}
+
+        def round_w1(b, a, on_vector):
+            bf = keep.tile([P, PACK * PASS], BF16, name=f"w1_bf{b}{a}", tag="bf", bufs=4, align_bytes=64)
+            dst = bf[:].rearrange("p (t m j) -> p m j t", t=PACK, j=PACK)
+            src = w1_raw[b, a][:].rearrange("p j (m t) -> p m j t", t=PACK)
+            if on_vector:
+                nc.vector.tensor_copy(out=dst, in_=src)
+            else:
+                nc.scalar.activation(out=dst, in_=src, func=ACT.Copy)
+            return bf
+
+        def quantise(bf, name):
+            codes = keep.tile([P, COLS], U32, name=f"{name}_codes", align_bytes=64)
+            scales = keep.tile([P, COLS], U8, name=f"{name}_scales", align_bytes=64)
+            nc.vector.quantize_mx(out=codes[:].bitcast(FP8X4), scales=scales[:], in_=bf[:])
+            return codes, scales
+
+        h_sb = {}
+
+        def h_block(b, t, c):
+            if (b, t) not in h_sb:
+                h_sb[b, t] = keep.tile([P, S], F32, name=f"h{b}{t}", tag="h", bufs=6, align_bytes=64)
+            bank = psum.tile([P, COLS], F32, name="bank", tag="bank")
+            cols = slice(c * COLS, (c + 1) * COLS)
+            for a in range(2):
+                codes, scales = w1_q[b, a]
+                moving = v0[:, cols] if a == 0 else v1[c][:]
+                nc.tensor.matmul_mx(
+                    out=bank[:],
+                    lhsT=codes[:, t * P:(t + 1) * P].bitcast(FP8X4),
+                    lhsT_scale=scales[:, t * P:(t + 1) * P],
+                    rhs=moving.bitcast(FP8X4),
+                    rhs_scale=v_sc[4 * a:P, cols],
+                    start=(a == 0), stop=(a == 1))
+            nc.scalar.activation(out=h_sb[b, t][:, cols], in_=bank[:], func=ACT.Copy)
+
+        x_sb = {}
+
+        def pick(b, t, half):
+            if (b, half) not in x_sb:
+                x_sb[b, half] = keep.tile([P, PACK, COLS], F32, name=f"x{b}{half}", align_bytes=64)
+            nc.vector.tensor_tensor(
+                x_sb[b, half][:, t, :],
+                h_sb[b, t][:].indirect(idx2[:, half * 32:(half + 1) * 32]),
+                wgt_sb[:, half * COLS:(half + 1) * COLS], ALU.mult)
+
+        def round_z(b, half, engines):
+            bf = keep.tile([P, PACK * COLS], BF16, name=f"z_bf{b}{half}", tag="bf", bufs=4, align_bytes=64)
+            dst = bf[:].rearrange("p (c i t) -> p c t i", i=4, t=PACK)
+            src = x_sb[b, half][:].rearrange("p t (c i) -> p c t i", i=4)
+            n = COLS // 4 // len(engines)
+            for k, engine in enumerate(engines):
+                part = slice(k * n, (k + 1) * n)
+                if engine == "V":
+                    nc.vector.tensor_scalar(dst[:, part], src[:, part], 0.0, None, ALU.max)
+                else:
+                    nc.scalar.activation(out=dst[:, part], in_=src[:, part], func=ACT.Relu)
+            z_q[b, half] = quantise(bf, f"z{b}{half}")
+
+        def scores(half, engines):
+            for nt in range(N // P):
+                bank = psum.tile([P, COLS], F32, name="bank", tag="bank")
+                for b in range(2):
+                    codes, scales = z_q[b, half]
+                    nc.tensor.matmul_mx(
+                        out=bank[:],
+                        lhsT=w2_wd[:, b, 2 * P * nt:2 * P * (nt + 1)].bitcast(FP4X4),
+                        lhsT_scale=w2_sc[:, b * N + nt * P:b * N + (nt + 1) * P],
+                        rhs=codes[:].bitcast(FP8X4),
+                        rhs_scale=scales[:],
+                        start=(b == 0), stop=(b == 1))
+                res = keep.tile([P, COLS], F32, name=f"res{half}{nt}", align_bytes=64)
+                if engines[nt] == "V":
+                    nc.vector.tensor_copy(out=res[:], in_=bank[:])
+                else:
+                    nc.scalar.activation(out=res[:], in_=bank[:], func=ACT.Copy)
+                nc.sync.dma_start(out=out[nt * P:(nt + 1) * P, half * COLS:(half + 1) * COLS], in_=res[:])
+
+        z_q = {}
+
+        nc.vector.tensor_copy(v_sc[:], table_sc[:].indirect(idx[:]))
+        v0 = keep.tile([P, S], U32, name="v0", tag="sc_then_v0", align_bytes=64)
+        nc.vector.tensor_copy(v0[:], table[0][:].bitcast(U32).indirect(idx[:]))
+        for a in range(2):
+            w1_q[0, a] = quantise(round_w1(0, a, False), f"w1_0{a}")
+        for c in range(4):
+            nc.vector.tensor_copy(v1[c][:], table[1][:].bitcast(U32).indirect(idx[:, c * 32:(c + 1) * 32]))
+            h_block(0, 0, c)
+            h_block(0, 1, c)
+        w1_q[1, 0] = quantise(round_w1(1, 0, True), "w1_10")
+        pick(0, 0, 0)
+        pick(0, 0, 1)
+        w1_q[1, 1] = quantise(round_w1(1, 1, False), "w1_11")
+        pick(0, 1, 0)
+        pick(0, 1, 1)
+        for t in (2, 3):
+            for c in range(4):
+                h_block(0, t, c)
+            pick(0, t, 0)
+            pick(0, t, 1)
+        for t in range(4):
+            for c in range(4):
+                h_block(1, t, c)
+            pick(1, t, 0)
+            if t < 3:
+                pick(1, t, 1)
+            if t == 1:
+                round_z(0, 1, "S")
+        round_z(0, 0, "SV")
+        round_z(1, 0, "S")
+        pick(1, 3, 1)
+        scores(0, "SSS")
+        round_z(1, 1, "SV")
+        scores(1, "SVS")

@@ -32,54 +32,56 @@ def tile_list_premise_selection_kernel(tc, tab_words, tab_scales, offs, w1, offs
         idx = lists.tile([P, S // 16], U16, name="idx")
         idx2 = lists.tile([P, G // 16], U16, name="idx2")
 
-        table = [keep.tile([P, T], I32, name=f"table{a}", align_bytes=64) for a in range(2)]
-        table_sc = keep.tile([P, T], U8, name="table_sc", tag="sc_then_v0", align_bytes=64)
-        w2_sc = keep.tile([P, 2 * N], U8, name="w2_sc", align_bytes=64)
-        w2_wd = keep.tile([P, 2, 2 * N], U8, name="w2_wd", align_bytes=64)
-        wgt_sb = keep.tile([P, G], F32, name="wgt_sb", align_bytes=64)
+        table = [keep.tile([P, T], I32, name=f"table{a}", tag=f"table{a}", align_bytes=64) for a in range(2)]
+        table_sc = keep.tile([P, T], U8, name="table_sc", tag="sc_then_wgt", align_bytes=64)
+        v_sc = keep.tile([P, 2 * S], U8, name="v_sc", align_bytes=64)
+        picked_sc = keep.tile([P, S], U8, name="picked_sc", align_bytes=64)
         w1_raw = {}
-        for b in range(2):
-            for a in range(2):
-                w1_raw[b, a] = keep.tile([P, PACK, PASS], F32, name=f"w1_raw{b}{a}", align_bytes=64)
+        for a in range(2):
+            w1_raw[0, a] = keep.tile([P, PACK * PASS], F32, name=f"w1_raw0{a}", tag=f"raw{a}", align_bytes=64)
 
-        nc.vector.memset(table_sc[:].bitcast(I32), 0)
-        nc.vector.memset(w2_sc[:].bitcast(I32), 0)
+        nc.vector.memset(table_sc[32:64, :].bitcast(I32), 0)
+        nc.vector.memset(table_sc[64:P, :].bitcast(I32), 0)
+        nc.vector.memset(v_sc[:].bitcast(I32), 0)
 
         def load_w1(b, a):
             rows = w1[a * PASS:(a + 1) * PASS, b * PASS:(b + 1) * PASS]
-            nc.sync.dma_start(out=w1_raw[b, a][:], in_=rows.rearrange("(p j) c -> p j c", j=PACK))
+            nc.sync.dma_start(out=w1_raw[b, a].rearrange("p (j c) -> p j c", j=PACK),
+                              in_=rows.rearrange("(p j) c -> p j c", j=PACK))
 
         def load_table(a):
             nc.sync.dma_start(out=table[a][:], in_=tab_words[a].rearrange("p t i -> p (t i)").bitcast(I32))
 
         nc.sync.dma_start(idx[:], offs)
-        load_table(0)
         for a in range(2):
-            for q in range(4):
-                nc.scalar.dma_start(out=table_sc[32 * q + 4 * a:32 * q + 4 * a + 4, :].bitcast(I32),
-                                    in_=tab_scales[a, 4 * q:4 * q + 4, :].bitcast(I32))
+            nc.sync.dma_start(out=table_sc[a:32:2, :].bitcast(I32), in_=tab_scales[a].bitcast(I32))
+        load_table(0)
+        w1_raw[0, 0] = w1_raw[0, 0][:]
+        w1_raw[0, 1] = w1_raw[0, 1][:]
         load_w1(0, 0)
         load_w1(0, 1)
         load_table(1)
         nc.sync.dma_start(idx2[:], offs2)
-        nc.sync.dma_start(out=wgt_sb[:], in_=wgt)
-        load_w1(1, 0)
-        load_w1(1, 1)
-        nc.sync.dma_start(out=w2_wd[:].bitcast(I32), in_=w2_words.rearrange("a p c -> p a c").bitcast(I32))
-        for q in range(4):
-            nc.sync.dma_start(
-                out=w2_sc[32 * q:32 * q + 4, :].rearrange("r (a n) -> r a n", a=2).bitcast(I32),
-                in_=w2_scales[:, 4 * q:4 * q + 4, :].rearrange("a r n -> r a n").bitcast(I32))
 
-        v_sc = keep.tile([P, S], U8, name="v_sc", align_bytes=64)
+        nc.vector.tensor_copy(picked_sc[:], table_sc[:].indirect(idx[:]))
+        for q in range(4):
+            nc.sync.dma_start(out=v_sc[32 * q:32 * q + 4, :].bitcast(I32),
+                              in_=picked_sc[8 * q:8 * q + 8, :].bitcast(I32))
+        v0 = keep.tile([P, S], U32, name="v0", align_bytes=64)
+        nc.vector.tensor_copy(v0[:], table[0][:].bitcast(U32).indirect(idx[:]))
         v1 = [keep.tile([P, COLS], U32, name=f"v1_{c}", align_bytes=64) for c in range(S // COLS)]
+
+        w1_late = keep.tile([P, 2 * PACK * PASS], F32, name="w1_late", tag="table0", align_bytes=64)
+        wgt_sb = keep.tile([P, G], F32, name="wgt_sb", tag="sc_then_wgt", align_bytes=64)
+        for a in range(2):
+            w1_raw[1, a] = w1_late[:, a * PACK * PASS:(a + 1) * PACK * PASS]
 
         w1_q = {}
 
         def round_w1(b, a, on_vector):
             bf = keep.tile([P, PACK * PASS], BF16, name=f"w1_bf{b}{a}", tag="bf", bufs=4, align_bytes=64)
             dst = bf[:].rearrange("p (t m j) -> p m j t", t=PACK, j=PACK)
-            src = w1_raw[b, a][:].rearrange("p j (m t) -> p m j t", t=PACK)
+            src = w1_raw[b, a].rearrange("p (j m t) -> p m j t", j=PACK, t=PACK)
             if on_vector:
                 nc.vector.tensor_copy(out=dst, in_=src)
             else:
@@ -107,7 +109,7 @@ def tile_list_premise_selection_kernel(tc, tab_words, tab_scales, offs, w1, offs
                     lhsT=codes[:, t * P:(t + 1) * P].bitcast(FP8X4),
                     lhsT_scale=scales[:, t * P:(t + 1) * P],
                     rhs=moving.bitcast(FP8X4),
-                    rhs_scale=v_sc[4 * a:P, cols],
+                    rhs_scale=v_sc[:, a * S + c * COLS:a * S + (c + 1) * COLS],
                     start=(a == 0), stop=(a == 1))
             nc.scalar.activation(out=h_sb[b, t][:, cols], in_=bank[:], func=ACT.Copy)
 
@@ -155,11 +157,19 @@ def tile_list_premise_selection_kernel(tc, tab_words, tab_scales, offs, w1, offs
 
         z_q = {}
 
-        nc.vector.tensor_copy(v_sc[:], table_sc[:].indirect(idx[:]))
-        v0 = keep.tile([P, S], U32, name="v0", tag="sc_then_v0", align_bytes=64)
-        nc.vector.tensor_copy(v0[:], table[0][:].bitcast(U32).indirect(idx[:]))
+        nc.sync.dma_start(out=wgt_sb[:], in_=wgt)
+        load_w1(1, 0)
+        load_w1(1, 1)
         for a in range(2):
             w1_q[0, a] = quantise(round_w1(0, a, False), f"w1_0{a}")
+        w2_wd = keep.tile([P, 2, 2 * N], U8, name="w2_wd", tag="raw0", align_bytes=64)
+        w2_sc = keep.tile([P, 2 * N], U8, name="w2_sc", tag="raw1", align_bytes=64)
+        nc.sync.dma_start(out=w2_wd[:].bitcast(I32), in_=w2_words.rearrange("a p c -> p a c").bitcast(I32))
+        nc.gpsimd.memset(w2_sc[:].bitcast(I32), 0)
+        for q in range(4):
+            nc.sync.dma_start(
+                out=w2_sc[32 * q:32 * q + 4, :].rearrange("r (a n) -> r a n", a=2).bitcast(I32),
+                in_=w2_scales[:, 4 * q:4 * q + 4, :].rearrange("a r n -> r a n").bitcast(I32))
         for c in range(4):
             nc.vector.tensor_copy(v1[c][:], table[1][:].bitcast(U32).indirect(idx[:, c * 32:(c + 1) * 32]))
             h_block(0, 0, c)

@@ -20,6 +20,8 @@ P = 128
 PACK = 4
 PASS = P * PACK
 COLS = 512
+HALF = G // 2
+QUARTER = G // 4
 
 
 def tile_list_premise_selection_kernel(tc, tab_words, tab_scales, offs, w1, offs2, wgt, w2_words, w2_scales, out):
@@ -29,76 +31,96 @@ def tile_list_premise_selection_kernel(tc, tab_words, tab_scales, offs, w1, offs
         keep = ctx.enter_context(tc.tile_pool(name="keep", bufs=1))
         psum = ctx.enter_context(tc.psum_pool(name="psum", bufs=8))
 
+        def sbuf(shape, dtype, name, slot=None, bufs=1):
+            return keep.tile(shape, dtype, name=name, tag=slot or name, bufs=bufs, align_bytes=64)
+
         idx = lists.tile([P, S // 16], U16, name="idx")
         idx2 = lists.tile([P, G // 16], U16, name="idx2")
 
-        table = [keep.tile([P, T], I32, name=f"table{a}", tag=f"table{a}", align_bytes=64) for a in range(2)]
-        table_sc = keep.tile([P, T], U8, name="table_sc", tag="sc_then_wgt", align_bytes=64)
-        v_sc = keep.tile([P, 2 * S], U8, name="v_sc", align_bytes=64)
-        picked_sc = keep.tile([P, S], U8, name="picked_sc", align_bytes=64)
+        table_sc = sbuf([P, T], U8, "table_sc", "slot_a")
+        table0 = sbuf([P, T], I32, "table0", "slot_b")
+        picked_sc = sbuf([P, S], U8, "picked_sc", "slot_c")
+        v_sc = [sbuf([P, S], U8, f"v_sc{a}") for a in range(2)]
         w1_raw = {}
-        for a in range(2):
-            w1_raw[0, a] = keep.tile([P, PACK * PASS], F32, name=f"w1_raw0{a}", tag=f"raw{a}", align_bytes=64)
+        w1_raw[0, 0] = sbuf([P, PACK * PASS], F32, "w1_raw00", "slot_d")[:]
+        w1_raw[0, 1] = sbuf([P, PACK * PASS], F32, "w1_raw01", "slot_e")[:]
 
         nc.vector.memset(table_sc[32:64, :].bitcast(I32), 0)
         nc.vector.memset(table_sc[64:P, :].bitcast(I32), 0)
-        nc.vector.memset(v_sc[:].bitcast(I32), 0)
+        for a in range(2):
+            nc.vector.memset(v_sc[a][:].bitcast(I32), 0)
 
         def load_w1(b, a):
             rows = w1[a * PASS:(a + 1) * PASS, b * PASS:(b + 1) * PASS]
             nc.sync.dma_start(out=w1_raw[b, a].rearrange("p (j c) -> p j c", j=PACK),
                               in_=rows.rearrange("(p j) c -> p j c", j=PACK))
 
-        def load_table(a):
-            nc.sync.dma_start(out=table[a][:], in_=tab_words[a].rearrange("p t i -> p (t i)").bitcast(I32))
+        def load_table(tile, a):
+            nc.sync.dma_start(out=tile[:], in_=tab_words[a].rearrange("p t i -> p (t i)").bitcast(I32))
+
+        def place_scales(a):
+            for q in (0, 2, 1, 3):
+                nc.sync.dma_start(out=v_sc[a][32 * q + 4 * a:32 * q + 4 * a + 4, :].bitcast(I32),
+                                  in_=picked_sc[16 * a + 4 * q:16 * a + 4 * q + 4, :].bitcast(I32))
 
         nc.sync.dma_start(idx[:], offs)
-        for a in range(2):
-            nc.sync.dma_start(out=table_sc[a:32:2, :].bitcast(I32), in_=tab_scales[a].bitcast(I32))
-        load_table(0)
-        w1_raw[0, 0] = w1_raw[0, 0][:]
-        w1_raw[0, 1] = w1_raw[0, 1][:]
+        nc.sync.dma_start(out=table_sc[0:32, :].bitcast(I32),
+                          in_=tab_scales.rearrange("a q t -> (a q) t").bitcast(I32))
+        load_table(table0, 0)
         load_w1(0, 0)
         load_w1(0, 1)
-        load_table(1)
         nc.sync.dma_start(idx2[:], offs2)
 
         nc.vector.tensor_copy(picked_sc[:], table_sc[:].indirect(idx[:]))
-        for q in range(4):
-            nc.sync.dma_start(out=v_sc[32 * q:32 * q + 4, :].bitcast(I32),
-                              in_=picked_sc[8 * q:8 * q + 8, :].bitcast(I32))
-        v0 = keep.tile([P, S], U32, name="v0", align_bytes=64)
-        nc.vector.tensor_copy(v0[:], table[0][:].bitcast(U32).indirect(idx[:]))
-        v1 = [keep.tile([P, COLS], U32, name=f"v1_{c}", align_bytes=64) for c in range(S // COLS)]
+        place_scales(0)
+        table1 = sbuf([P, T], I32, "table1", "slot_a")
+        load_table(table1, 1)
+        place_scales(1)
 
-        w1_late = keep.tile([P, 2 * PACK * PASS], F32, name="w1_late", tag="table0", align_bytes=64)
-        wgt_sb = keep.tile([P, G], F32, name="wgt_sb", tag="sc_then_wgt", align_bytes=64)
+        v0 = sbuf([P, S], U32, "v0")
+        nc.vector.tensor_copy(v0[:], table0[:].bitcast(U32).indirect(idx[:]))
+        w1_late = sbuf([P, 2 * PACK * PASS], F32, "w1_late", "slot_b")
         for a in range(2):
             w1_raw[1, a] = w1_late[:, a * PACK * PASS:(a + 1) * PACK * PASS]
+            load_w1(1, a)
 
-        w1_q = {}
-
-        def round_w1(b, a, on_vector):
-            bf = keep.tile([P, PACK * PASS], BF16, name=f"w1_bf{b}{a}", tag="bf", bufs=4, align_bytes=64)
-            dst = bf[:].rearrange("p (t m j) -> p m j t", t=PACK, j=PACK)
-            src = w1_raw[b, a].rearrange("p (j m t) -> p m j t", j=PACK, t=PACK)
-            if on_vector:
-                nc.vector.tensor_copy(out=dst, in_=src)
-            else:
-                nc.scalar.activation(out=dst, in_=src, func=ACT.Copy)
-            return bf
-
-        def quantise(bf, name):
-            codes = keep.tile([P, COLS], U32, name=f"{name}_codes", align_bytes=64)
-            scales = keep.tile([P, COLS], U8, name=f"{name}_scales", align_bytes=64)
+        def quantise(bf, width, name):
+            codes = sbuf([P, width], U32, f"{name}_codes")
+            scales = sbuf([P, width], U8, f"{name}_scales")
             nc.vector.quantize_mx(out=codes[:].bitcast(FP8X4), scales=scales[:], in_=bf[:])
             return codes, scales
 
+        w1_q = {}
+
+        def prepare_w1(b, a, engine):
+            bf = sbuf([P, PACK * PASS], BF16, f"w1_bf{b}{a}", "bf", 4)
+            dst = bf[:].rearrange("p (t m j) -> p m j t", t=PACK, j=PACK)
+            src = w1_raw[b, a].rearrange("p (j m t) -> p m j t", j=PACK, t=PACK)
+            if engine == "V":
+                nc.vector.tensor_copy(out=dst, in_=src)
+            else:
+                nc.scalar.activation(out=dst, in_=src, func=ACT.Copy)
+            w1_q[b, a] = quantise(bf, PASS, f"w1_{b}{a}")
+
+        wgt_sb = []
+        for a, slot in enumerate(("slot_d", "slot_e")):
+            prepare_w1(0, a, "S")
+            wgt_sb.append(sbuf([P, HALF], F32, f"wgt{a}", slot))
+            nc.sync.dma_start(out=wgt_sb[a][:], in_=wgt[:, a * HALF:(a + 1) * HALF])
+
+        w2_sc = sbuf([P, 2 * N], U8, "w2_sc", "slot_c")
+        nc.gpsimd.memset(w2_sc[:].bitcast(I32), 0)
+        for q in range(4):
+            nc.sync.dma_start(
+                out=w2_sc[32 * q:32 * q + 4, :].rearrange("r (a n) -> r a n", a=2).bitcast(I32),
+                in_=w2_scales[:, 4 * q:4 * q + 4, :].rearrange("a r n -> r a n").bitcast(I32))
+
+        v1 = [sbuf([P, COLS], U32, f"v1_{c}") for c in range(S // COLS)]
         h_sb = {}
 
         def h_block(b, t, c):
             if (b, t) not in h_sb:
-                h_sb[b, t] = keep.tile([P, S], F32, name=f"h{b}{t}", tag="h", bufs=6, align_bytes=64)
+                h_sb[b, t] = sbuf([P, S], F32, f"h{b}{t}", "h", 6)
             bank = psum.tile([P, COLS], F32, name="bank", tag="bank")
             cols = slice(c * COLS, (c + 1) * COLS)
             for a in range(2):
@@ -109,93 +131,90 @@ def tile_list_premise_selection_kernel(tc, tab_words, tab_scales, offs, w1, offs
                     lhsT=codes[:, t * P:(t + 1) * P].bitcast(FP8X4),
                     lhsT_scale=scales[:, t * P:(t + 1) * P],
                     rhs=moving.bitcast(FP8X4),
-                    rhs_scale=v_sc[:, a * S + c * COLS:a * S + (c + 1) * COLS],
+                    rhs_scale=v_sc[a][4 * a:P, cols],
                     start=(a == 0), stop=(a == 1))
             nc.scalar.activation(out=h_sb[b, t][:, cols], in_=bank[:], func=ACT.Copy)
 
         x_sb = {}
 
-        def pick(b, t, half):
-            if (b, half) not in x_sb:
-                x_sb[b, half] = keep.tile([P, PACK, COLS], F32, name=f"x{b}{half}", align_bytes=64)
+        def pick(b, t, m0, width, slot=None):
+            if (b, m0) not in x_sb:
+                x_sb[b, m0] = sbuf([P, PACK, width], F32, f"x{b}_{m0}", slot)
+            w0 = m0 % HALF
             nc.vector.tensor_tensor(
-                x_sb[b, half][:, t, :],
-                h_sb[b, t][:].indirect(idx2[:, half * 32:(half + 1) * 32]),
-                wgt_sb[:, half * COLS:(half + 1) * COLS], ALU.mult)
+                x_sb[b, m0][:, t, :],
+                h_sb[b, t][:].indirect(idx2[:, m0 // 16:(m0 + width) // 16]),
+                wgt_sb[m0 // HALF][:, w0:w0 + width], ALU.mult)
 
-        def round_z(b, half, engines):
-            bf = keep.tile([P, PACK * COLS], BF16, name=f"z_bf{b}{half}", tag="bf", bufs=4, align_bytes=64)
+        z_q = {}
+
+        def prepare_z(b, m0, width, engines, slot="bf", bufs=4):
+            bf = sbuf([P, PACK * width], BF16, f"z_bf{b}_{m0}", slot, bufs)
             dst = bf[:].rearrange("p (c i t) -> p c t i", i=4, t=PACK)
-            src = x_sb[b, half][:].rearrange("p t (c i) -> p c t i", i=4)
-            n = COLS // 4 // len(engines)
+            src = x_sb[b, m0][:].rearrange("p t (c i) -> p c t i", i=4)
+            n = width // 4 // len(engines)
             for k, engine in enumerate(engines):
                 part = slice(k * n, (k + 1) * n)
                 if engine == "V":
                     nc.vector.tensor_scalar(dst[:, part], src[:, part], 0.0, None, ALU.max)
                 else:
                     nc.scalar.activation(out=dst[:, part], in_=src[:, part], func=ACT.Relu)
-            z_q[b, half] = quantise(bf, f"z{b}{half}")
+            z_q[b, m0] = quantise(bf, width, f"z{b}_{m0}")
 
-        def scores(half, engines):
+        def scores(m0, width, engines):
+            step = COLS if width == COLS else P
             for nt in range(N // P):
                 bank = psum.tile([P, COLS], F32, name="bank", tag="bank")
                 for b in range(2):
-                    codes, scales = z_q[b, half]
-                    nc.tensor.matmul_mx(
-                        out=bank[:],
-                        lhsT=w2_wd[:, b, 2 * P * nt:2 * P * (nt + 1)].bitcast(FP4X4),
-                        lhsT_scale=w2_sc[:, b * N + nt * P:b * N + (nt + 1) * P],
-                        rhs=codes[:].bitcast(FP8X4),
-                        rhs_scale=scales[:],
-                        start=(b == 0), stop=(b == 1))
-                res = keep.tile([P, COLS], F32, name=f"res{half}{nt}", align_bytes=64)
+                    base = m0 if (b, m0) in z_q else m0 // HALF * HALF
+                    codes, scales = z_q[b, base]
+                    for c0 in range(0, width, step):
+                        cols = slice(m0 - base + c0, m0 - base + c0 + step)
+                        nc.tensor.matmul_mx(
+                            out=bank[:, c0:c0 + step],
+                            lhsT=w2_wd[:, b, 2 * P * nt:2 * P * (nt + 1)].bitcast(FP4X4),
+                            lhsT_scale=w2_sc[:, b * N + nt * P:b * N + (nt + 1) * P],
+                            rhs=codes[:, cols].bitcast(FP8X4),
+                            rhs_scale=scales[:, cols],
+                            start=(b == 0 and c0 == 0), stop=(b == 1 and c0 + step == width))
+                res = sbuf([P, width], F32, f"res{m0}_{nt}")
                 if engines[nt] == "V":
-                    nc.vector.tensor_copy(out=res[:], in_=bank[:])
+                    nc.vector.tensor_copy(out=res[:], in_=bank[:, 0:width])
                 else:
-                    nc.scalar.activation(out=res[:], in_=bank[:], func=ACT.Copy)
-                nc.sync.dma_start(out=out[nt * P:(nt + 1) * P, half * COLS:(half + 1) * COLS], in_=res[:])
+                    nc.scalar.activation(out=res[:], in_=bank[:, 0:width], func=ACT.Copy)
+                nc.sync.dma_start(out=out[nt * P:(nt + 1) * P, m0:m0 + width], in_=res[:])
 
-        z_q = {}
-
-        nc.sync.dma_start(out=wgt_sb[:], in_=wgt)
-        load_w1(1, 0)
-        load_w1(1, 1)
-        for a in range(2):
-            w1_q[0, a] = quantise(round_w1(0, a, False), f"w1_0{a}")
-        w2_wd = keep.tile([P, 2, 2 * N], U8, name="w2_wd", tag="raw0", align_bytes=64)
-        w2_sc = keep.tile([P, 2 * N], U8, name="w2_sc", tag="raw1", align_bytes=64)
-        nc.sync.dma_start(out=w2_wd[:].bitcast(I32), in_=w2_words.rearrange("a p c -> p a c").bitcast(I32))
-        nc.gpsimd.memset(w2_sc[:].bitcast(I32), 0)
-        for q in range(4):
-            nc.sync.dma_start(
-                out=w2_sc[32 * q:32 * q + 4, :].rearrange("r (a n) -> r a n", a=2).bitcast(I32),
-                in_=w2_scales[:, 4 * q:4 * q + 4, :].rearrange("a r n -> r a n").bitcast(I32))
-        for c in range(4):
-            nc.vector.tensor_copy(v1[c][:], table[1][:].bitcast(U32).indirect(idx[:, c * 32:(c + 1) * 32]))
+        for c in range(S // COLS):
+            nc.vector.tensor_copy(v1[c][:], table1[:].bitcast(U32).indirect(idx[:, c * 32:(c + 1) * 32]))
             h_block(0, 0, c)
             h_block(0, 1, c)
-        w1_q[1, 0] = quantise(round_w1(1, 0, True), "w1_10")
-        pick(0, 0, 0)
-        pick(0, 0, 1)
-        w1_q[1, 1] = quantise(round_w1(1, 1, False), "w1_11")
-        pick(0, 1, 0)
-        pick(0, 1, 1)
+        w2_wd = sbuf([P, 2, 2 * N], U8, "w2_wd", "slot_a")
+        nc.sync.dma_start(out=w2_wd[:].bitcast(I32), in_=w2_words.rearrange("a p c -> p a c").bitcast(I32))
+
+        prepare_w1(1, 0, "V")
+        pick(0, 0, 0, HALF)
+        pick(0, 0, HALF, HALF)
+        prepare_w1(1, 1, "S")
+        pick(0, 1, 0, HALF)
+        pick(0, 1, HALF, HALF)
         for t in (2, 3):
-            for c in range(4):
+            for c in range(S // COLS):
                 h_block(0, t, c)
-            pick(0, t, 0)
-            pick(0, t, 1)
-        for t in range(4):
-            for c in range(4):
+            pick(0, t, 0, HALF)
+            pick(0, t, HALF, HALF)
+        for t in range(PACK):
+            for c in range(S // COLS):
                 h_block(1, t, c)
-            pick(1, t, 0)
-            if t < 3:
-                pick(1, t, 1)
-            if t == 1:
-                round_z(0, 1, "S")
-        round_z(0, 0, "SV")
-        round_z(1, 0, "S")
-        pick(1, 3, 1)
-        scores(0, "SSS")
-        round_z(1, 1, "SV")
-        scores(1, "SVS")
+            pick(1, t, 0, HALF)
+        prepare_z(0, 0, HALF, "SV")
+        prepare_z(1, 0, HALF, "S", "slot_f", 1)
+        for t in range(PACK):
+            pick(1, t, HALF, QUARTER, "slot_d")
+        prepare_z(0, HALF, HALF, "SV")
+        scores(0, HALF, "SSS")
+        prepare_z(1, HALF, QUARTER, "S")
+        for t in range(PACK):
+            pick(1, t, HALF + QUARTER, QUARTER, "slot_f")
+        scores(HALF, QUARTER, "SSS")
+        prepare_z(1, HALF + QUARTER, QUARTER, "V")
+        scores(HALF + QUARTER, QUARTER, "SVS")

@@ -148,18 +148,22 @@ def tile_list_premise_selection_kernel(tc, tab_words, tab_scales, offs, w1, offs
 
         z_q = {}
 
-        def prepare_z(b, m0, width, engines, slot="bf", bufs=4):
-            bf = sbuf([P, PACK * width], BF16, f"z_bf{b}_{m0}", slot, bufs)
-            dst = bf[:].rearrange("p (c i t) -> p c t i", i=4, t=PACK)
-            src = x_sb[b, m0][:].rearrange("p t (c i) -> p c t i", i=4)
-            n = width // 4 // len(engines)
-            for k, engine in enumerate(engines):
-                part = slice(k * n, (k + 1) * n)
-                if engine == "V":
-                    nc.vector.tensor_scalar(dst[:, part], src[:, part], 0.0, None, ALU.max)
-                else:
-                    nc.scalar.activation(out=dst[:, part], in_=src[:, part], func=ACT.Relu)
-            z_q[b, m0] = quantise(bf, width, f"z{b}_{m0}")
+        z_bf = {}
+
+        def round_z(b, m0, width, engine, part=0, parts=1, slot="bf", bufs=4):
+            if (b, m0) not in z_bf:
+                z_bf[b, m0] = sbuf([P, PACK * width], BF16, f"z_bf{b}_{m0}", slot, bufs)
+            n = width // 4 // parts
+            share = slice(part * n, (part + 1) * n)
+            dst = z_bf[b, m0][:].rearrange("p (c i t) -> p c t i", i=4, t=PACK)[:, share]
+            src = x_sb[b, m0][:].rearrange("p t (c i) -> p c t i", i=4)[:, share]
+            if engine == "V":
+                nc.vector.tensor_scalar(dst, src, 0.0, None, ALU.max)
+            else:
+                nc.scalar.activation(out=dst, in_=src, func=ACT.Relu)
+
+        def quantise_z(b, m0, width):
+            z_q[b, m0] = quantise(z_bf[b, m0], width, f"z{b}_{m0}")
 
         def scores(m0, width, engines):
             step = COLS if width == COLS else P
@@ -202,19 +206,25 @@ def tile_list_premise_selection_kernel(tc, tab_words, tab_scales, offs, w1, offs
                 h_block(0, t, c)
             pick(0, t, 0, HALF)
             pick(0, t, HALF, HALF)
+        round_z(0, 0, HALF, "V")
+        quantise_z(0, 0, HALF)
         for t in range(PACK):
             for c in range(S // COLS):
                 h_block(1, t, c)
             pick(1, t, 0, HALF)
-        prepare_z(0, 0, HALF, "SV")
-        prepare_z(1, 0, HALF, "S", "slot_f", 1)
+        round_z(0, HALF, HALF, "S", 0, 2)
+        round_z(1, 0, HALF, "S", slot="slot_f", bufs=1)
+        quantise_z(1, 0, HALF)
         for t in range(PACK):
             pick(1, t, HALF, QUARTER, "slot_d")
-        prepare_z(0, HALF, HALF, "SV")
+        round_z(0, HALF, HALF, "S", 1, 2)
+        quantise_z(0, HALF, HALF)
+        round_z(1, HALF, QUARTER, "S")
+        quantise_z(1, HALF, QUARTER)
         scores(0, HALF, "SSS")
-        prepare_z(1, HALF, QUARTER, "S")
         for t in range(PACK):
             pick(1, t, HALF + QUARTER, QUARTER, "slot_f")
         scores(HALF, QUARTER, "SSS")
-        prepare_z(1, HALF + QUARTER, QUARTER, "V")
+        round_z(1, HALF + QUARTER, QUARTER, "V")
+        quantise_z(1, HALF + QUARTER, QUARTER)
         scores(HALF + QUARTER, QUARTER, "SVS")

@@ -29,21 +29,27 @@ def tile_list_premise_selection_kernel(tc, tab_words, tab_scales, offs, w1, offs
     with ExitStack() as ctx:
         lists = ctx.enter_context(tc.tile_pool(name="lists", bufs=1))
         keep = ctx.enter_context(tc.tile_pool(name="keep", bufs=1))
-        psum = ctx.enter_context(tc.psum_pool(name="psum", bufs=8))
+        psum = ctx.enter_context(tc.psum_pool(name="psum", bufs=1))
 
         def sbuf(shape, dtype, name, slot=None, bufs=1):
             return keep.tile(shape, dtype, name=name, tag=slot or name, bufs=bufs, align_bytes=64)
+
+        opened = []
+
+        def bank():
+            opened.append(psum.tile([P, COLS], F32, name="bank", tag=f"bank{len(opened) % 8}"))
+            return opened[-1]
 
         idx = lists.tile([P, S // 16], U16, name="idx")
         idx2 = lists.tile([P, G // 16], U16, name="idx2")
 
         table_sc = sbuf([P, T], U8, "table_sc", "slot_a")
         table0 = sbuf([P, T], I32, "table0", "slot_b")
+        table1 = sbuf([P, T], I32, "table1", "slot_t")
         picked_sc = sbuf([P, S], U8, "picked_sc", "slot_c")
         v_sc = [sbuf([P, S], U8, f"v_sc{a}") for a in range(2)]
         w1_raw = {}
         w1_raw[0, 0] = sbuf([P, PACK * PASS], F32, "w1_raw00", "slot_d")[:]
-        w1_raw[0, 1] = sbuf([P, PACK * PASS], F32, "w1_raw01", "slot_e")[:]
 
         nc.vector.memset(table_sc[32:64, :].bitcast(I32), 0)
         nc.vector.memset(table_sc[64:P, :].bitcast(I32), 0)
@@ -68,95 +74,105 @@ def tile_list_premise_selection_kernel(tc, tab_words, tab_scales, offs, w1, offs
                           in_=tab_scales.rearrange("a q t -> (a q) t").bitcast(I32))
         load_table(table0, 0)
         load_w1(0, 0)
-        load_w1(0, 1)
+        load_table(table1, 1)
         nc.sync.dma_start(idx2[:], offs2)
 
         nc.vector.tensor_copy(picked_sc[:], table_sc[:].indirect(idx[:]))
         place_scales(0)
-        table1 = sbuf([P, T], I32, "table1", "slot_a")
-        load_table(table1, 1)
+        w1_raw[0, 1] = sbuf([P, PACK * PASS], F32, "w1_raw01", "slot_a")[:]
+        load_w1(0, 1)
         place_scales(1)
 
         v0 = sbuf([P, S], U32, "v0")
         nc.vector.tensor_copy(v0[:], table0[:].bitcast(U32).indirect(idx[:]))
-        w1_late = sbuf([P, 2 * PACK * PASS], F32, "w1_late", "slot_b")
-        for a in range(2):
-            w1_raw[1, a] = w1_late[:, a * PACK * PASS:(a + 1) * PACK * PASS]
-            load_w1(1, a)
 
         def quantise(bf, width, name):
-            codes = sbuf([P, width], U32, f"{name}_codes")
+            codes = sbuf([P, width], U32, f"{name}_codes", f"slot_{name}")
             scales = sbuf([P, width], U8, f"{name}_scales")
             nc.vector.quantize_mx(out=codes[:].bitcast(FP8X4), scales=scales[:], in_=bf[:])
             return codes, scales
 
         w1_q = {}
+        w1_bf = {}
 
-        def prepare_w1(b, a, engine):
-            bf = sbuf([P, PACK * PASS], BF16, f"w1_bf{b}{a}", "bf", 4)
-            dst = bf[:].rearrange("p (t m j) -> p m j t", t=PACK, j=PACK)
-            src = w1_raw[b, a].rearrange("p (j m t) -> p m j t", j=PACK, t=PACK)
+        def round_w1(b, a, engine, t0=0, n=PACK, slot="bf", bufs=4):
+            bf = sbuf([P, n * PASS], BF16, f"w1_bf{b}{a}{t0}", slot, bufs)
+            dst = bf[:].rearrange("p (t m j) -> p m j t", t=n, j=PACK)
+            src = w1_raw[b, a].rearrange("p (j m t) -> p m j t", j=PACK, t=PACK)[:, :, :, t0:t0 + n]
             if engine == "V":
                 nc.vector.tensor_copy(out=dst, in_=src)
             else:
                 nc.scalar.activation(out=dst, in_=src, func=ACT.Copy)
-            w1_q[b, a] = quantise(bf, PASS, f"w1_{b}{a}")
+            w1_bf[b, a, t0] = bf
 
-        wgt_sb = []
-        for a, slot in enumerate(("slot_d", "slot_e")):
-            prepare_w1(0, a, "S")
-            wgt_sb.append(sbuf([P, HALF], F32, f"wgt{a}", slot))
-            nc.sync.dma_start(out=wgt_sb[a][:], in_=wgt[:, a * HALF:(a + 1) * HALF])
+        def quantise_w1(b, a, t0=0, n=PACK):
+            codes, scales = quantise(w1_bf[b, a, t0], n * P, f"w1_{b}{a}{t0}")
+            for t in range(n):
+                w1_q[b, a, t0 + t] = codes[:, t * P:(t + 1) * P], scales[:, t * P:(t + 1) * P]
 
-        w2_sc = sbuf([P, 2 * N], U8, "w2_sc", "slot_c")
-        nc.gpsimd.memset(w2_sc[:].bitcast(I32), 0)
-        for q in range(4):
-            nc.sync.dma_start(
-                out=w2_sc[32 * q:32 * q + 4, :].rearrange("r (a n) -> r a n", a=2).bitcast(I32),
-                in_=w2_scales[:, 4 * q:4 * q + 4, :].rearrange("a r n -> r a n").bitcast(I32))
+        round_w1(0, 0, "S")
+        quantise_w1(0, 0)
 
-        v1 = [sbuf([P, COLS], U32, f"v1_{c}") for c in range(S // COLS)]
+        w1_raw[1, 0] = sbuf([P, PACK * PASS], F32, "w1_raw10", "slot_b")[:]
+        w1_raw[1, 1] = sbuf([P, PACK * PASS], F32, "w1_raw11", "slot_c")[:]
+        for a in range(2):
+            load_w1(1, a)
+        wgt_sb = sbuf([P, G], F32, "wgt_sb", "slot_d")
+        nc.sync.dma_start(out=wgt_sb[:], in_=wgt)
+
+        v1 = {}
         h_sb = {}
+        banks = {}
 
-        def h_block(b, t, c):
-            if (b, t) not in h_sb:
-                h_sb[b, t] = sbuf([P, S], F32, f"h{b}{t}", "h", 6)
-            bank = psum.tile([P, COLS], F32, name="bank", tag="bank")
+        def gather_v1(c, slot=None):
+            v1[c] = sbuf([P, COLS], U32, f"v1_{c}", slot)
+            nc.vector.tensor_copy(v1[c][:], table1[:].bitcast(U32).indirect(idx[:, c * 32:(c + 1) * 32]))
+
+        def h_pass(b, t, c, a):
+            if a == 0:
+                banks[b, t, c] = bank()
             cols = slice(c * COLS, (c + 1) * COLS)
-            for a in range(2):
-                codes, scales = w1_q[b, a]
-                moving = v0[:, cols] if a == 0 else v1[c][:]
-                nc.tensor.matmul_mx(
-                    out=bank[:],
-                    lhsT=codes[:, t * P:(t + 1) * P].bitcast(FP8X4),
-                    lhsT_scale=scales[:, t * P:(t + 1) * P],
-                    rhs=moving.bitcast(FP8X4),
-                    rhs_scale=v_sc[a][4 * a:P, cols],
-                    start=(a == 0), stop=(a == 1))
-            nc.scalar.activation(out=h_sb[b, t][:, cols], in_=bank[:], func=ACT.Copy)
+            codes, scales = w1_q[b, a, t]
+            moving = v0[:, cols] if a == 0 else v1[c][:]
+            nc.tensor.matmul_mx(
+                out=banks[b, t, c][:],
+                lhsT=codes.bitcast(FP8X4), lhsT_scale=scales,
+                rhs=moving.bitcast(FP8X4), rhs_scale=v_sc[a][4 * a:P, cols],
+                start=(a == 0), stop=(a == 1))
+
+        def h_copy(b, t, c, engine="S"):
+            if (b, t) not in h_sb:
+                h_sb[b, t] = sbuf([P, S], F32, f"h{b}{t}", f"h{(PACK * b + t) % 6}")
+            dst = h_sb[b, t][:, c * COLS:(c + 1) * COLS]
+            if engine == "V":
+                nc.vector.tensor_copy(out=dst, in_=banks[b, t, c][:])
+            else:
+                nc.scalar.activation(out=dst, in_=banks[b, t, c][:], func=ACT.Copy)
+
+        def h_tile(b, t):
+            for c in range(S // COLS):
+                h_pass(b, t, c, 0)
+                h_pass(b, t, c, 1)
+                h_copy(b, t, c)
 
         x_sb = {}
 
         def pick(b, t, m0, width, slot=None):
             if (b, m0) not in x_sb:
                 x_sb[b, m0] = sbuf([P, PACK, width], F32, f"x{b}_{m0}", slot)
-            w0 = m0 % HALF
             nc.vector.tensor_tensor(
                 x_sb[b, m0][:, t, :],
                 h_sb[b, t][:].indirect(idx2[:, m0 // 16:(m0 + width) // 16]),
-                wgt_sb[m0 // HALF][:, w0:w0 + width], ALU.mult)
+                wgt_sb[:, m0:m0 + width], ALU.mult)
 
         z_q = {}
-
         z_bf = {}
 
-        def round_z(b, m0, width, engine, part=0, parts=1, slot="bf", bufs=4):
-            if (b, m0) not in z_bf:
-                z_bf[b, m0] = sbuf([P, PACK * width], BF16, f"z_bf{b}_{m0}", slot, bufs)
-            n = width // 4 // parts
-            share = slice(part * n, (part + 1) * n)
-            dst = z_bf[b, m0][:].rearrange("p (c i t) -> p c t i", i=4, t=PACK)[:, share]
-            src = x_sb[b, m0][:].rearrange("p t (c i) -> p c t i", i=4)[:, share]
+        def round_z(b, m0, width, engine, slot="bf", bufs=4):
+            base = max(m for bb, m in x_sb if bb == b and m <= m0)
+            z_bf[b, m0] = sbuf([P, PACK * width], BF16, f"z_bf{b}_{m0}", slot, bufs)
+            dst = z_bf[b, m0][:].rearrange("p (c i t) -> p c t i", i=4, t=PACK)
+            src = x_sb[b, base][:, :, m0 - base:m0 - base + width].rearrange("p t (c i) -> p c t i", i=4)
             if engine == "V":
                 nc.vector.tensor_scalar(dst, src, 0.0, None, ALU.max)
             else:
@@ -167,64 +183,84 @@ def tile_list_premise_selection_kernel(tc, tab_words, tab_scales, offs, w1, offs
 
         def scores(m0, width, engines):
             step = COLS if width == COLS else P
-            for nt in range(N // P):
-                bank = psum.tile([P, COLS], F32, name="bank", tag="bank")
-                for b in range(2):
-                    base = m0 if (b, m0) in z_q else m0 // HALF * HALF
-                    codes, scales = z_q[b, base]
+            acc = [bank() for nt in range(N // P)]
+            for b in range(2):
+                base = m0 if (b, m0) in z_q else m0 // HALF * HALF
+                codes, scales = z_q[b, base]
+                for nt in range(N // P):
                     for c0 in range(0, width, step):
                         cols = slice(m0 - base + c0, m0 - base + c0 + step)
                         nc.tensor.matmul_mx(
-                            out=bank[:, c0:c0 + step],
+                            out=acc[nt][:, c0:c0 + step],
                             lhsT=w2_wd[:, b, 2 * P * nt:2 * P * (nt + 1)].bitcast(FP4X4),
                             lhsT_scale=w2_sc[:, b * N + nt * P:b * N + (nt + 1) * P],
                             rhs=codes[:, cols].bitcast(FP8X4),
                             rhs_scale=scales[:, cols],
                             start=(b == 0 and c0 == 0), stop=(b == 1 and c0 + step == width))
-                res = sbuf([P, width], F32, f"res{m0}_{nt}")
+            res = sbuf([P, N // P, width], F32, f"res{m0}")
+            rows = out[:, m0:m0 + width].rearrange("(nt p) m -> p nt m", p=P)
+            for nt in range(N // P):
                 if engines[nt] == "V":
-                    nc.vector.tensor_copy(out=res[:], in_=bank[:, 0:width])
+                    nc.vector.tensor_copy(out=res[:, nt, :], in_=acc[nt][:, 0:width])
                 else:
-                    nc.scalar.activation(out=res[:], in_=bank[:, 0:width], func=ACT.Copy)
-                nc.sync.dma_start(out=out[nt * P:(nt + 1) * P, m0:m0 + width], in_=res[:])
+                    nc.scalar.activation(out=res[:, nt, :], in_=acc[nt][:, 0:width], func=ACT.Copy)
+                if width > P:
+                    nc.sync.dma_start(out=rows[:, nt, :], in_=res[:, nt, :])
+            if width == P:
+                nc.sync.dma_start(out=rows, in_=res[:])
 
-        for c in range(S // COLS):
-            nc.vector.tensor_copy(v1[c][:], table1[:].bitcast(U32).indirect(idx[:, c * 32:(c + 1) * 32]))
-            h_block(0, 0, c)
-            h_block(0, 1, c)
-        w2_wd = sbuf([P, 2, 2 * N], U8, "w2_wd", "slot_a")
+        for t in range(2):
+            for c in range(S // COLS):
+                h_pass(0, t, c, 0)
+        for c in range(3):
+            gather_v1(c)
+        round_w1(0, 1, "S", 0, 2, "slot_g", 1)
+        quantise_w1(0, 1, 0, 2)
+        gather_v1(3, "slot_g")
+        w2_wd = sbuf([P, 2, 2 * N], U8, "w2_wd", "slot_t")
         nc.sync.dma_start(out=w2_wd[:].bitcast(I32), in_=w2_words.rearrange("a p c -> p a c").bitcast(I32))
-
-        prepare_w1(1, 0, "V")
-        pick(0, 0, 0, HALF)
-        pick(0, 0, HALF, HALF)
-        prepare_w1(1, 1, "S")
-        pick(0, 1, 0, HALF)
-        pick(0, 1, HALF, HALF)
-        for t in (2, 3):
+        round_w1(0, 1, "S", 2, 2)
+        quantise_w1(0, 1, 2, 2)
+        w2_sc = sbuf([P, 2 * N], U8, "w2_sc", "slot_a")
+        nc.gpsimd.memset(w2_sc[:].bitcast(I32), 0)
+        for q in range(4):
+            nc.sync.dma_start(
+                out=w2_sc[32 * q:32 * q + 4, :].rearrange("r (a n) -> r a n", a=2).bitcast(I32),
+                in_=w2_scales[:, 4 * q:4 * q + 4, :].rearrange("a r n -> r a n").bitcast(I32))
+        for t in range(2):
             for c in range(S // COLS):
-                h_block(0, t, c)
-            pick(0, t, 0, HALF)
-            pick(0, t, HALF, HALF)
-        round_z(0, 0, HALF, "V")
-        quantise_z(0, 0, HALF)
+                h_pass(0, t, c, 1)
+                h_copy(0, t, c)
+        round_w1(1, 0, "V")
+        quantise_w1(1, 0)
+        round_w1(1, 1, "V", slot="slot_x", bufs=1)
+        quantise_w1(1, 1)
         for t in range(PACK):
-            for c in range(S // COLS):
-                h_block(1, t, c)
+            if t > 1:
+                h_tile(0, t)
+            pick(0, t, 0, G, "slot_x")
+        for t in range(PACK):
+            h_tile(1, t)
             pick(1, t, 0, HALF)
-        round_z(0, HALF, HALF, "S", 0, 2)
+        round_z(0, 0, HALF, "S", slot="slot_g", bufs=1)
+        quantise_z(0, 0, HALF)
         round_z(1, 0, HALF, "S", slot="slot_f", bufs=1)
         quantise_z(1, 0, HALF)
-        for t in range(PACK):
-            pick(1, t, HALF, QUARTER, "slot_d")
-        round_z(0, HALF, HALF, "S", 1, 2)
+        round_z(0, HALF, HALF, "S", slot="slot_w1_110", bufs=1)
         quantise_z(0, HALF, HALF)
-        round_z(1, HALF, QUARTER, "S")
-        quantise_z(1, HALF, QUARTER)
         scores(0, HALF, "SSS")
         for t in range(PACK):
-            pick(1, t, HALF + QUARTER, QUARTER, "slot_f")
+            pick(1, t, HALF, QUARTER, "slot_g")
+        round_z(1, HALF, QUARTER, "S")
+        quantise_z(1, HALF, QUARTER)
+        for t in range(PACK):
+            pick(1, t, G - 2 * P, P, "slot_f")
+        round_z(1, G - 2 * P, P, "S")
+        quantise_z(1, G - 2 * P, P)
+        for t in range(PACK):
+            pick(1, t, G - P, P, "slot_w1_110")
         scores(HALF, QUARTER, "SSS")
-        round_z(1, HALF + QUARTER, QUARTER, "V")
-        quantise_z(1, HALF + QUARTER, QUARTER)
-        scores(HALF + QUARTER, QUARTER, "SVS")
+        scores(G - 2 * P, P, "SSS")
+        round_z(1, G - P, P, "V")
+        quantise_z(1, G - P, P)
+        scores(G - P, P, "VSV")

@@ -56,10 +56,14 @@ def tile_list_premise_selection_kernel(tc, tab_words, tab_scales, offs, w1, offs
         for a in range(2):
             nc.vector.memset(v_sc[a][:].bitcast(I32), 0)
 
-        def load_w1(b, a):
+        warm = sbuf([P, 2], F32, "warm")
+        nc.vector.memset(warm[:, 0:1], 0.0)
+        nc.scalar.activation(out=warm[:, 1:2], in_=warm[:, 0:1], func=ACT.Copy)
+
+        def load_w1(b, a, j0=0, n=PACK):
             rows = w1[a * PASS:(a + 1) * PASS, b * PASS:(b + 1) * PASS]
-            nc.sync.dma_start(out=w1_raw[b, a].rearrange("p (j c) -> p j c", j=PACK),
-                              in_=rows.rearrange("(p j) c -> p j c", j=PACK))
+            nc.sync.dma_start(out=w1_raw[b, a].rearrange("p (j c) -> p j c", j=PACK)[:, j0:j0 + n, :],
+                              in_=rows.rearrange("(p j) c -> p j c", j=PACK)[:, j0:j0 + n, :])
 
         def load_table(tile, a):
             nc.sync.dma_start(out=tile[:], in_=tab_words[a].rearrange("p t i -> p (t i)").bitcast(I32))
@@ -73,8 +77,9 @@ def tile_list_premise_selection_kernel(tc, tab_words, tab_scales, offs, w1, offs
         nc.sync.dma_start(out=table_sc[0:32, :].bitcast(I32),
                           in_=tab_scales.rearrange("a q t -> (a q) t").bitcast(I32))
         load_table(table0, 0)
-        load_w1(0, 0)
+        load_w1(0, 0, 0, 2)
         load_table(table1, 1)
+        load_w1(0, 0, 2, 2)
         nc.sync.dma_start(idx2[:], offs2)
 
         nc.vector.tensor_copy(picked_sc[:], table_sc[:].indirect(idx[:]))
@@ -110,30 +115,29 @@ def tile_list_premise_selection_kernel(tc, tab_words, tab_scales, offs, w1, offs
             for t in range(n):
                 w1_q[b, a, t0 + t] = codes[:, t * P:(t + 1) * P], scales[:, t * P:(t + 1) * P]
 
-        round_w1(0, 0, "S")
-        quantise_w1(0, 0)
-
-        w1_raw[1, 0] = sbuf([P, PACK * PASS], F32, "w1_raw10", "slot_b")[:]
-        w1_raw[1, 1] = sbuf([P, PACK * PASS], F32, "w1_raw11", "slot_c")[:]
+        late = sbuf([P, 2 * PACK * PASS], F32, "late", "slot_b")
         for a in range(2):
+            w1_raw[1, a] = late[:, a * PACK * PASS:(a + 1) * PACK * PASS]
             load_w1(1, a)
-        wgt_sb = sbuf([P, G], F32, "wgt_sb", "slot_d")
+        wgt_sb = sbuf([P, G], F32, "wgt_sb", "slot_c")
         nc.sync.dma_start(out=wgt_sb[:], in_=wgt)
 
         v1 = {}
         h_sb = {}
         banks = {}
 
-        def gather_v1(c, slot=None):
-            v1[c] = sbuf([P, COLS], U32, f"v1_{c}", slot)
-            nc.vector.tensor_copy(v1[c][:], table1[:].bitcast(U32).indirect(idx[:, c * 32:(c + 1) * 32]))
+        def gather_v1(u, slot=None):
+            half = sbuf([P, S // 2], U32, f"v1_{u}", slot)
+            nc.vector.tensor_copy(half[:], table1[:].bitcast(U32).indirect(idx[:, u * 64:(u + 1) * 64]))
+            for c in range(2):
+                v1[2 * u + c] = half[:, c * COLS:(c + 1) * COLS]
 
         def h_pass(b, t, c, a):
             if a == 0:
                 banks[b, t, c] = bank()
             cols = slice(c * COLS, (c + 1) * COLS)
             codes, scales = w1_q[b, a, t]
-            moving = v0[:, cols] if a == 0 else v1[c][:]
+            moving = v0[:, cols] if a == 0 else v1[c]
             nc.tensor.matmul_mx(
                 out=banks[b, t, c][:],
                 lhsT=codes.bitcast(FP8X4), lhsT_scale=scales,
@@ -209,16 +213,18 @@ def tile_list_premise_selection_kernel(tc, tab_words, tab_scales, offs, w1, offs
             if width == P:
                 nc.sync.dma_start(out=rows, in_=res[:])
 
-        for t in range(2):
-            for c in range(S // COLS):
-                h_pass(0, t, c, 0)
-        for c in range(3):
-            gather_v1(c)
-        round_w1(0, 1, "S", 0, 2, "slot_g", 1)
-        quantise_w1(0, 1, 0, 2)
-        gather_v1(3, "slot_g")
+        gather_v1(0)
+        round_w1(0, 0, "S", 0, 2, "slot_g", 1)
+        quantise_w1(0, 0, 0, 2)
+        for c in range(S // COLS):
+            h_pass(0, 0, c, 0)
+        gather_v1(1, "slot_g")
         w2_wd = sbuf([P, 2, 2 * N], U8, "w2_wd", "slot_t")
         nc.sync.dma_start(out=w2_wd[:].bitcast(I32), in_=w2_words.rearrange("a p c -> p a c").bitcast(I32))
+        round_w1(0, 0, "S", 2, 2)
+        round_w1(0, 1, "S", 0, 2)
+        quantise_w1(0, 1, 0, 2)
+        quantise_w1(0, 0, 2, 2)
         round_w1(0, 1, "S", 2, 2)
         quantise_w1(0, 1, 2, 2)
         w2_sc = sbuf([P, 2 * N], U8, "w2_sc", "slot_a")
@@ -227,40 +233,37 @@ def tile_list_premise_selection_kernel(tc, tab_words, tab_scales, offs, w1, offs
             nc.sync.dma_start(
                 out=w2_sc[32 * q:32 * q + 4, :].rearrange("r (a n) -> r a n", a=2).bitcast(I32),
                 in_=w2_scales[:, 4 * q:4 * q + 4, :].rearrange("a r n -> r a n").bitcast(I32))
-        for t in range(2):
-            for c in range(S // COLS):
-                h_pass(0, t, c, 1)
-                h_copy(0, t, c)
+        for c in range(S // COLS):
+            h_pass(0, 0, c, 1)
+            h_copy(0, 0, c)
         round_w1(1, 0, "V")
         quantise_w1(1, 0)
         round_w1(1, 1, "V", slot="slot_x", bufs=1)
         quantise_w1(1, 1)
         for t in range(PACK):
-            if t > 1:
+            if t > 0:
                 h_tile(0, t)
             pick(0, t, 0, G, "slot_x")
         for t in range(PACK):
             h_tile(1, t)
-            pick(1, t, 0, HALF)
+            pick(1, t, 0, G - QUARTER)
         round_z(0, 0, HALF, "S", slot="slot_g", bufs=1)
         quantise_z(0, 0, HALF)
-        round_z(1, 0, HALF, "S", slot="slot_f", bufs=1)
-        quantise_z(1, 0, HALF)
         round_z(0, HALF, HALF, "S", slot="slot_w1_110", bufs=1)
         quantise_z(0, HALF, HALF)
-        scores(0, HALF, "SSS")
-        for t in range(PACK):
-            pick(1, t, HALF, QUARTER, "slot_g")
+        round_z(1, 0, HALF, "S", slot="slot_f", bufs=1)
+        quantise_z(1, 0, HALF)
         round_z(1, HALF, QUARTER, "S")
         quantise_z(1, HALF, QUARTER)
         for t in range(PACK):
-            pick(1, t, G - 2 * P, P, "slot_f")
+            pick(1, t, G - 2 * P, P, "slot_w1_110")
         round_z(1, G - 2 * P, P, "S")
         quantise_z(1, G - 2 * P, P)
+        scores(0, HALF, "SSS")
         for t in range(PACK):
-            pick(1, t, G - P, P, "slot_w1_110")
+            pick(1, t, G - P, P, "slot_f")
         scores(HALF, QUARTER, "SSS")
-        scores(G - 2 * P, P, "SSS")
+        scores(G - 2 * P, P, "VVV")
         round_z(1, G - P, P, "V")
         quantise_z(1, G - P, P)
-        scores(G - P, P, "VSV")
+        scores(G - P, P, "VVS")

@@ -49,21 +49,23 @@ def tile_list_premise_selection_kernel(tc, tab_words, tab_scales, offs, w1, offs
         picked_sc = sbuf([P, S], U8, "picked_sc", "slot_c")
         v_sc = [sbuf([P, S], U8, f"v_sc{a}") for a in range(2)]
         w1_raw = {}
-        w1_raw[0, 0] = sbuf([P, PACK * PASS], F32, "w1_raw00", "slot_d")[:]
 
         nc.vector.memset(table_sc[32:64, :].bitcast(I32), 0)
         nc.vector.memset(table_sc[64:P, :].bitcast(I32), 0)
         for a in range(2):
             nc.vector.memset(v_sc[a][:].bitcast(I32), 0)
 
-        warm = sbuf([P, 2], F32, "warm")
-        nc.vector.memset(warm[:, 0:1], 0.0)
-        nc.scalar.activation(out=warm[:, 1:2], in_=warm[:, 0:1], func=ACT.Copy)
-
-        def load_w1(b, a, j0=0, n=PACK):
-            rows = w1[a * PASS:(a + 1) * PASS, b * PASS:(b + 1) * PASS]
-            nc.sync.dma_start(out=w1_raw[b, a].rearrange("p (j c) -> p j c", j=PACK)[:, j0:j0 + n, :],
-                              in_=rows.rearrange("(p j) c -> p j c", j=PACK)[:, j0:j0 + n, :])
+        def load_w1(pieces, slot=None):
+            total = sum(PASS // parts for b, a, part, parts in pieces)
+            tile = sbuf([P, PACK * total], F32, "w1_raw%d%d%d" % pieces[0][:3], slot)
+            at = 0
+            for b, a, part, parts in pieces:
+                width = PASS // parts
+                w1_raw[b, a, part] = tile[:, at:at + PACK * width]
+                at = at + PACK * width
+                c0 = b * PASS + part * width
+                nc.sync.dma_start(out=w1_raw[b, a, part].rearrange("p (j c) -> p j c", j=PACK),
+                                  in_=w1[a * PASS:(a + 1) * PASS, c0:c0 + width].rearrange("(p j) c -> p j c", j=PACK))
 
         def load_table(tile, a):
             nc.sync.dma_start(out=tile[:], in_=tab_words[a].rearrange("p t i -> p (t i)").bitcast(I32))
@@ -77,18 +79,16 @@ def tile_list_premise_selection_kernel(tc, tab_words, tab_scales, offs, w1, offs
         nc.sync.dma_start(out=table_sc[0:32, :].bitcast(I32),
                           in_=tab_scales.rearrange("a q t -> (a q) t").bitcast(I32))
         load_table(table0, 0)
-        load_w1(0, 0, 0, 2)
+        load_w1([(0, 0, 0, 2)])
         load_table(table1, 1)
-        load_w1(0, 0, 2, 2)
         nc.sync.dma_start(idx2[:], offs2)
 
         nc.vector.tensor_copy(picked_sc[:], table_sc[:].indirect(idx[:]))
         place_scales(0)
-        w1_raw[0, 1] = sbuf([P, PACK * PASS], F32, "w1_raw01", "slot_a")[:]
-        load_w1(0, 1)
+        load_w1([(0, 0, 1, 2), (0, 1, 0, 2), (0, 1, 1, 2)], "slot_a")
         place_scales(1)
 
-        v0 = sbuf([P, S], U32, "v0")
+        v0 = sbuf([P, S], U32, "v0", "slot_v0")
         nc.vector.tensor_copy(v0[:], table0[:].bitcast(U32).indirect(idx[:]))
 
         def quantise(bf, width, name):
@@ -100,25 +100,23 @@ def tile_list_premise_selection_kernel(tc, tab_words, tab_scales, offs, w1, offs
         w1_q = {}
         w1_bf = {}
 
-        def round_w1(b, a, engine, t0=0, n=PACK, slot="bf", bufs=4):
-            bf = sbuf([P, n * PASS], BF16, f"w1_bf{b}{a}{t0}", slot, bufs)
-            dst = bf[:].rearrange("p (t m j) -> p m j t", t=n, j=PACK)
-            src = w1_raw[b, a].rearrange("p (j m t) -> p m j t", j=PACK, t=PACK)[:, :, :, t0:t0 + n]
+        def round_w1(b, a, engine, t0=0, n=PACK, slot="bf", bufs=4, part=0, parts=1):
+            if part == 0:
+                w1_bf[b, a, t0] = sbuf([P, n * PASS], BF16, f"w1_bf{b}{a}{t0}", slot, bufs)
+            share = slice(part * P // parts, (part + 1) * P // parts)
+            dst = w1_bf[b, a, t0][:].rearrange("p (t m j) -> p m j t", t=n, j=PACK)[:, share]
+            src = w1_raw[b, a, part].rearrange("p (j m t) -> p m j t", j=PACK, t=PACK)[:, :, :, t0:t0 + n]
             if engine == "V":
                 nc.vector.tensor_copy(out=dst, in_=src)
             else:
                 nc.scalar.activation(out=dst, in_=src, func=ACT.Copy)
-            w1_bf[b, a, t0] = bf
 
         def quantise_w1(b, a, t0=0, n=PACK):
             codes, scales = quantise(w1_bf[b, a, t0], n * P, f"w1_{b}{a}{t0}")
             for t in range(n):
                 w1_q[b, a, t0 + t] = codes[:, t * P:(t + 1) * P], scales[:, t * P:(t + 1) * P]
 
-        late = sbuf([P, 2 * PACK * PASS], F32, "late", "slot_b")
-        for a in range(2):
-            w1_raw[1, a] = late[:, a * PACK * PASS:(a + 1) * PACK * PASS]
-            load_w1(1, a)
+        load_w1([(1, 0, 0, 1), (1, 1, 0, 1)], "slot_b")
         wgt_sb = sbuf([P, G], F32, "wgt_sb", "slot_c")
         nc.sync.dma_start(out=wgt_sb[:], in_=wgt)
 
@@ -126,14 +124,15 @@ def tile_list_premise_selection_kernel(tc, tab_words, tab_scales, offs, w1, offs
         h_sb = {}
         banks = {}
 
-        def gather_v1(u, slot=None):
-            half = sbuf([P, S // 2], U32, f"v1_{u}", slot)
-            nc.vector.tensor_copy(half[:], table1[:].bitcast(U32).indirect(idx[:, u * 64:(u + 1) * 64]))
-            for c in range(2):
-                v1[2 * u + c] = half[:, c * COLS:(c + 1) * COLS]
+        def gather_v1(c0, n, slot=None):
+            part = sbuf([P, n * COLS], U32, f"v1_{c0}", slot)
+            nc.vector.tensor_copy(part[:], table1[:].bitcast(U32).indirect(idx[:, c0 * 32:(c0 + n) * 32]))
+            for c in range(n):
+                v1[c0 + c] = part[:, c * COLS:(c + 1) * COLS]
 
         def h_pass(b, t, c, a):
-            if a == 0:
+            first = (b, t, c) not in banks
+            if first:
                 banks[b, t, c] = bank()
             cols = slice(c * COLS, (c + 1) * COLS)
             codes, scales = w1_q[b, a, t]
@@ -142,7 +141,7 @@ def tile_list_premise_selection_kernel(tc, tab_words, tab_scales, offs, w1, offs
                 out=banks[b, t, c][:],
                 lhsT=codes.bitcast(FP8X4), lhsT_scale=scales,
                 rhs=moving.bitcast(FP8X4), rhs_scale=v_sc[a][4 * a:P, cols],
-                start=(a == 0), stop=(a == 1))
+                start=first, stop=not first)
 
         def h_copy(b, t, c, engine="S"):
             if (b, t) not in h_sb:
@@ -155,8 +154,8 @@ def tile_list_premise_selection_kernel(tc, tab_words, tab_scales, offs, w1, offs
 
         def h_tile(b, t):
             for c in range(S // COLS):
-                h_pass(b, t, c, 0)
                 h_pass(b, t, c, 1)
+                h_pass(b, t, c, 0)
                 h_copy(b, t, c)
 
         x_sb = {}
@@ -213,50 +212,57 @@ def tile_list_premise_selection_kernel(tc, tab_words, tab_scales, offs, w1, offs
             if width == P:
                 nc.sync.dma_start(out=rows, in_=res[:])
 
-        gather_v1(0)
-        round_w1(0, 0, "S", 0, 2, "slot_g", 1)
+        gather_v1(0, 2)
+        round_w1(0, 0, "S", 0, 2, "slot_g", 1, 0, 2)
+        round_w1(0, 0, "S", 2, 2, "bf", 4, 0, 2)
+        round_w1(0, 0, "S", 0, 2, "slot_g", 1, 1, 2)
         quantise_w1(0, 0, 0, 2)
-        for c in range(S // COLS):
+        for c in range(3):
             h_pass(0, 0, c, 0)
-        gather_v1(1, "slot_g")
+        gather_v1(2, 1, "slot_g")
+        round_w1(0, 0, "S", 2, 2, "bf", 4, 1, 2)
+        quantise_w1(0, 0, 2, 2)
+        round_w1(0, 1, "S", 0, 2, "slot_h", 1, 0, 2)
+        round_w1(0, 1, "S", 2, 2, "bf", 4, 0, 2)
+        round_w1(0, 1, "S", 0, 2, "slot_h", 1, 1, 2)
+        quantise_w1(0, 1, 0, 2)
+        gather_v1(3, 1, "slot_h")
         w2_wd = sbuf([P, 2, 2 * N], U8, "w2_wd", "slot_t")
         nc.sync.dma_start(out=w2_wd[:].bitcast(I32), in_=w2_words.rearrange("a p c -> p a c").bitcast(I32))
-        round_w1(0, 0, "S", 2, 2)
-        round_w1(0, 1, "S", 0, 2)
-        quantise_w1(0, 1, 0, 2)
-        quantise_w1(0, 0, 2, 2)
-        round_w1(0, 1, "S", 2, 2)
+        round_w1(0, 1, "S", 2, 2, "bf", 4, 1, 2)
         quantise_w1(0, 1, 2, 2)
         w2_sc = sbuf([P, 2 * N], U8, "w2_sc", "slot_a")
-        nc.gpsimd.memset(w2_sc[:].bitcast(I32), 0)
+        nc.vector.memset(w2_sc[:].bitcast(I32), 0)
         for q in range(4):
             nc.sync.dma_start(
                 out=w2_sc[32 * q:32 * q + 4, :].rearrange("r (a n) -> r a n", a=2).bitcast(I32),
                 in_=w2_scales[:, 4 * q:4 * q + 4, :].rearrange("a r n -> r a n").bitcast(I32))
         for c in range(S // COLS):
             h_pass(0, 0, c, 1)
+            if c == 3:
+                h_pass(0, 0, c, 0)
             h_copy(0, 0, c)
         round_w1(1, 0, "V")
         quantise_w1(1, 0)
-        round_w1(1, 1, "V", slot="slot_x", bufs=1)
+        round_w1(1, 1, "V")
+        pick(0, 0, 0, G, "slot_b")
         quantise_w1(1, 1)
-        for t in range(PACK):
-            if t > 0:
-                h_tile(0, t)
-            pick(0, t, 0, G, "slot_x")
+        for t in range(1, PACK):
+            h_tile(0, t)
+            pick(0, t, 0, G)
         for t in range(PACK):
             h_tile(1, t)
             pick(1, t, 0, G - QUARTER)
-        round_z(0, 0, HALF, "S", slot="slot_g", bufs=1)
+        round_z(0, 0, HALF, "S", slot="slot_v0", bufs=1)
         quantise_z(0, 0, HALF)
-        round_z(0, HALF, HALF, "S", slot="slot_w1_110", bufs=1)
+        round_z(0, HALF, HALF, "S", slot="slot_w1_100", bufs=1)
         quantise_z(0, HALF, HALF)
         round_z(1, 0, HALF, "S", slot="slot_f", bufs=1)
         quantise_z(1, 0, HALF)
         round_z(1, HALF, QUARTER, "S")
         quantise_z(1, HALF, QUARTER)
         for t in range(PACK):
-            pick(1, t, G - 2 * P, P, "slot_w1_110")
+            pick(1, t, G - 2 * P, P, "slot_w1_100")
         round_z(1, G - 2 * P, P, "S")
         quantise_z(1, G - 2 * P, P)
         scores(0, HALF, "SSS")

@@ -85,7 +85,7 @@ def tile_list_premise_selection_kernel(tc, tab_words, tab_scales, offs, w1, offs
 
         nc.vector.tensor_copy(picked_sc[:], table_sc[:].indirect(idx[:]))
         place_scales(0)
-        load_w1([(0, 0, 1, 2), (0, 1, 0, 2), (0, 1, 1, 2)], "slot_a")
+        load_w1([(0, 0, 1, 2), (0, 1, 0, 2), (0, 1, 2, 4), (0, 1, 3, 4)], "slot_a")
         place_scales(1)
 
         v0 = sbuf([P, S], U32, "v0", "slot_v0")
@@ -101,7 +101,7 @@ def tile_list_premise_selection_kernel(tc, tab_words, tab_scales, offs, w1, offs
         w1_bf = {}
 
         def round_w1(b, a, engine, t0=0, n=PACK, slot="bf", bufs=4, part=0, parts=1):
-            if part == 0:
+            if (b, a, t0) not in w1_bf:
                 w1_bf[b, a, t0] = sbuf([P, n * PASS], BF16, f"w1_bf{b}{a}{t0}", slot, bufs)
             share = slice(part * P // parts, (part + 1) * P // parts)
             dst = w1_bf[b, a, t0][:].rearrange("p (t m j) -> p m j t", t=n, j=PACK)[:, share]
@@ -116,9 +116,13 @@ def tile_list_premise_selection_kernel(tc, tab_words, tab_scales, offs, w1, offs
             for t in range(n):
                 w1_q[b, a, t0 + t] = codes[:, t * P:(t + 1) * P], scales[:, t * P:(t + 1) * P]
 
-        load_w1([(1, 0, 0, 1), (1, 1, 0, 1)], "slot_b")
-        wgt_sb = sbuf([P, G], F32, "wgt_sb", "slot_c")
-        nc.sync.dma_start(out=wgt_sb[:], in_=wgt)
+        after_table0 = sbuf([P, 2 * PACK * PASS + G], F32, "after_table0", "slot_b")
+        wgt_sb = after_table0[:, 2 * PACK * PASS:]
+        for a in range(2):
+            w1_raw[1, a, 0] = after_table0[:, a * PACK * PASS:(a + 1) * PACK * PASS]
+            nc.sync.dma_start(out=w1_raw[1, a, 0].rearrange("p (j c) -> p j c", j=PACK),
+                              in_=w1[a * PASS:(a + 1) * PASS, PASS:].rearrange("(p j) c -> p j c", j=PACK))
+            nc.sync.dma_start(out=wgt_sb[:, a * HALF:(a + 1) * HALF], in_=wgt[:, a * HALF:(a + 1) * HALF])
 
         v1 = {}
         h_sb = {}
@@ -160,11 +164,12 @@ def tile_list_premise_selection_kernel(tc, tab_words, tab_scales, offs, w1, offs
 
         x_sb = {}
 
-        def pick(b, t, m0, width, slot=None):
-            if (b, m0) not in x_sb:
-                x_sb[b, m0] = sbuf([P, PACK, width], F32, f"x{b}_{m0}", slot)
+        def pick(b, t, m0, width, slot=None, base=None, whole=None):
+            base = m0 if base is None else base
+            if (b, base) not in x_sb:
+                x_sb[b, base] = sbuf([P, PACK, whole or width], F32, f"x{b}_{base}", slot)
             nc.vector.tensor_tensor(
-                x_sb[b, m0][:, t, :],
+                x_sb[b, base][:, t, m0 - base:m0 - base + width],
                 h_sb[b, t][:].indirect(idx2[:, m0 // 16:(m0 + width) // 16]),
                 wgt_sb[:, m0:m0 + width], ALU.mult)
 
@@ -212,6 +217,9 @@ def tile_list_premise_selection_kernel(tc, tab_words, tab_scales, offs, w1, offs
             if width == P:
                 nc.sync.dma_start(out=rows, in_=res[:])
 
+        late_bf = sbuf([P, 2, 2 * PASS], BF16, "late_bf")
+        for a in range(2):
+            w1_bf[0, a, 2] = late_bf[:, a, :]
         gather_v1(0, 2)
         round_w1(0, 0, "S", 0, 2, "slot_g", 1, 0, 2)
         round_w1(0, 0, "S", 2, 2, "bf", 4, 0, 2)
@@ -221,18 +229,26 @@ def tile_list_premise_selection_kernel(tc, tab_words, tab_scales, offs, w1, offs
             h_pass(0, 0, c, 0)
         gather_v1(2, 1, "slot_g")
         round_w1(0, 0, "S", 2, 2, "bf", 4, 1, 2)
-        quantise_w1(0, 0, 2, 2)
         round_w1(0, 1, "S", 0, 2, "slot_h", 1, 0, 2)
-        round_w1(0, 1, "S", 2, 2, "bf", 4, 0, 2)
-        round_w1(0, 1, "S", 0, 2, "slot_h", 1, 1, 2)
+        round_w1(0, 1, "S", 0, 2, "slot_h", 1, 2, 4)
+        round_w1(0, 1, "S", 0, 2, "slot_h", 1, 3, 4)
         quantise_w1(0, 1, 0, 2)
         gather_v1(3, 1, "slot_h")
         w2_wd = sbuf([P, 2, 2 * N], U8, "w2_wd", "slot_t")
         nc.sync.dma_start(out=w2_wd[:].bitcast(I32), in_=w2_words.rearrange("a p c -> p a c").bitcast(I32))
-        round_w1(0, 1, "S", 2, 2, "bf", 4, 1, 2)
-        quantise_w1(0, 1, 2, 2)
+        round_w1(0, 1, "S", 2, 2, "bf", 4, 3, 4)
+        round_w1(0, 1, "S", 2, 2, "bf", 4, 2, 4)
+        round_w1(0, 1, "S", 2, 2, "bf", 4, 0, 2)
+        late_codes = sbuf([P, PASS], U32, "late_codes")
+        late_scales = sbuf([P, PASS], U8, "late_scales")
+        nc.vector.quantize_mx(out=late_codes[:].bitcast(FP8X4), scales=late_scales[:],
+                              in_=late_bf[:].rearrange("p a c -> p (a c)"))
+        for a in range(2):
+            for t in range(2, PACK):
+                cols = slice((2 * a + t - 2) * P, (2 * a + t - 1) * P)
+                w1_q[0, a, t] = late_codes[:, cols], late_scales[:, cols]
         w2_sc = sbuf([P, 2 * N], U8, "w2_sc", "slot_a")
-        nc.vector.memset(w2_sc[:].bitcast(I32), 0)
+        nc.gpsimd.memset(w2_sc[:].bitcast(I32), 0)
         for q in range(4):
             nc.sync.dma_start(
                 out=w2_sc[32 * q:32 * q + 4, :].rearrange("r (a n) -> r a n", a=2).bitcast(I32),
@@ -244,8 +260,9 @@ def tile_list_premise_selection_kernel(tc, tab_words, tab_scales, offs, w1, offs
             h_copy(0, 0, c)
         round_w1(1, 0, "V")
         quantise_w1(1, 0)
+        pick(0, 0, 0, HALF, whole=G)
         round_w1(1, 1, "V")
-        pick(0, 0, 0, G, "slot_b")
+        pick(0, 0, HALF, HALF, base=0)
         quantise_w1(1, 1)
         for t in range(1, PACK):
             h_tile(0, t)

@@ -32,7 +32,7 @@ def tile_list_premise_selection_kernel(tc, tab_words, tab_scales, offs, w1, offs
         psum = ctx.enter_context(tc.psum_pool(name="psum", bufs=1))
 
         def sbuf(shape, dtype, name, slot=None, bufs=1):
-            return keep.tile(shape, dtype, name=name, tag=slot or name, bufs=bufs, align_bytes=64)
+            return keep.tile(shape, dtype, name=name, tag=slot or name, bufs=bufs, align_bytes=256)
 
         opened = []
 
@@ -47,7 +47,7 @@ def tile_list_premise_selection_kernel(tc, tab_words, tab_scales, offs, w1, offs
         table0 = sbuf([P, T], I32, "table0", "slot_b")
         table1 = sbuf([P, T], I32, "table1", "slot_t")
         picked_sc = sbuf([P, S], U8, "picked_sc", "slot_c")
-        v_sc = [sbuf([P, S], U8, f"v_sc{a}") for a in range(2)]
+        v_sc = [sbuf([P, S + 64], U8, f"v_sc{a}")[:, 64:] for a in range(2)]
         w1_raw = {}
 
         nc.vector.memset(table_sc[32:64, :].bitcast(I32), 0)
@@ -92,8 +92,9 @@ def tile_list_premise_selection_kernel(tc, tab_words, tab_scales, offs, w1, offs
         nc.vector.tensor_copy(v0[:], table0[:].bitcast(U32).indirect(idx[:]))
 
         def quantise(bf, width, name):
-            codes = sbuf([P, width], U32, f"{name}_codes", f"slot_{name}")
-            scales = sbuf([P, width], U8, f"{name}_scales")
+            lead = (32, 192) if name.startswith("w1") else (0, 64)
+            codes = sbuf([P, width + lead[0]], U32, f"{name}_codes", f"slot_{name}")[:, lead[0]:]
+            scales = sbuf([P, width + lead[1]], U8, f"{name}_scales")[:, lead[1]:]
             nc.vector.quantize_mx(out=codes[:].bitcast(FP8X4), scales=scales[:], in_=bf[:])
             return codes, scales
 
@@ -239,8 +240,8 @@ def tile_list_premise_selection_kernel(tc, tab_words, tab_scales, offs, w1, offs
         round_w1(0, 1, "S", 2, 2, "bf", 4, 3, 4)
         round_w1(0, 1, "S", 2, 2, "bf", 4, 2, 4)
         round_w1(0, 1, "S", 2, 2, "bf", 4, 0, 2)
-        late_codes = sbuf([P, PASS], U32, "late_codes")
-        late_scales = sbuf([P, PASS], U8, "late_scales")
+        late_codes = sbuf([P, PASS + 32], U32, "late_codes")[:, 32:]
+        late_scales = sbuf([P, PASS + 192], U8, "late_scales")[:, 192:]
         nc.vector.quantize_mx(out=late_codes[:].bitcast(FP8X4), scales=late_scales[:],
                               in_=late_bf[:].rearrange("p a c -> p (a c)"))
         for a in range(2):

@@ -92,7 +92,7 @@ def tile_list_premise_selection_kernel(tc, tab_words, tab_scales, offs, w1, offs
         nc.vector.tensor_copy(v0[:], table0[:].bitcast(U32).indirect(idx[:]))
 
         def quantise(bf, width, name):
-            lead = (32, 192) if name.startswith("w1") else (0, 64)
+            lead = (48, 128) if name.startswith("w1") else (0, 64)
             codes = sbuf([P, width + lead[0]], U32, f"{name}_codes", f"slot_{name}")[:, lead[0]:]
             scales = sbuf([P, width + lead[1]], U8, f"{name}_scales")[:, lead[1]:]
             nc.vector.quantize_mx(out=codes[:].bitcast(FP8X4), scales=scales[:], in_=bf[:])
@@ -240,8 +240,8 @@ def tile_list_premise_selection_kernel(tc, tab_words, tab_scales, offs, w1, offs
         round_w1(0, 1, "S", 2, 2, "bf", 4, 3, 4)
         round_w1(0, 1, "S", 2, 2, "bf", 4, 2, 4)
         round_w1(0, 1, "S", 2, 2, "bf", 4, 0, 2)
-        late_codes = sbuf([P, PASS + 32], U32, "late_codes")[:, 32:]
-        late_scales = sbuf([P, PASS + 192], U8, "late_scales")[:, 192:]
+        late_codes = sbuf([P, PASS + 48], U32, "late_codes")[:, 48:]
+        late_scales = sbuf([P, PASS + 128], U8, "late_scales")[:, 128:]
         nc.vector.quantize_mx(out=late_codes[:].bitcast(FP8X4), scales=late_scales[:],
                               in_=late_bf[:].rearrange("p a c -> p (a c)"))
         for a in range(2):

@@ -22,6 +22,8 @@ PASS = P * PACK
 COLS = 512
 HALF = G // 2
 QUARTER = G // 4
+EARLY = [(0, 0), (0, 1), (0, 2), (0, 3), (1, 0)]
+WARM = 4
 
 
 def tile_list_premise_selection_kernel(tc, tab_words, tab_scales, offs, w1, offs2, wgt, w2_words, w2_scales, out):
@@ -90,6 +92,12 @@ def tile_list_premise_selection_kernel(tc, tab_words, tab_scales, offs, w1, offs
 
         v0 = sbuf([P, S], U32, "v0", "slot_v0")
         nc.vector.tensor_copy(v0[:], table0[:].bitcast(U32).indirect(idx[:]))
+
+        warm = psum.tile([P, COLS], F32, name="warm", tag="bank7")
+        for k in range(WARM):
+            nc.tensor.matmul_mx(
+                out=warm[:], lhsT=v0[:, 0:P].bitcast(FP8X4), lhsT_scale=v_sc[0][:, 0:P],
+                rhs=v0[:, 0:COLS].bitcast(FP8X4), rhs_scale=v_sc[0][:, 0:COLS], start=True, stop=True)
 
         def quantise(bf, width, name):
             lead = (48, 128) if name.startswith("w1") else (0, 64)
@@ -160,7 +168,8 @@ def tile_list_premise_selection_kernel(tc, tab_words, tab_scales, offs, w1, offs
         def h_tile(b, t):
             for c in range(S // COLS):
                 h_pass(b, t, c, 1)
-                h_pass(b, t, c, 0)
+                if b == 1 or (t, c) not in EARLY:
+                    h_pass(b, t, c, 0)
                 h_copy(b, t, c)
 
         x_sb = {}
@@ -226,8 +235,8 @@ def tile_list_premise_selection_kernel(tc, tab_words, tab_scales, offs, w1, offs
         round_w1(0, 0, "S", 2, 2, "bf", 4, 0, 2)
         round_w1(0, 0, "S", 0, 2, "slot_g", 1, 1, 2)
         quantise_w1(0, 0, 0, 2)
-        for c in range(3):
-            h_pass(0, 0, c, 0)
+        for t, c in EARLY:
+            h_pass(0, t, c, 0)
         gather_v1(2, 1, "slot_g")
         round_w1(0, 0, "S", 2, 2, "bf", 4, 1, 2)
         round_w1(0, 1, "S", 0, 2, "slot_h", 1, 0, 2)
@@ -254,11 +263,7 @@ def tile_list_premise_selection_kernel(tc, tab_words, tab_scales, offs, w1, offs
             nc.sync.dma_start(
                 out=w2_sc[32 * q:32 * q + 4, :].rearrange("r (a n) -> r a n", a=2).bitcast(I32),
                 in_=w2_scales[:, 4 * q:4 * q + 4, :].rearrange("a r n -> r a n").bitcast(I32))
-        for c in range(S // COLS):
-            h_pass(0, 0, c, 1)
-            if c == 3:
-                h_pass(0, 0, c, 0)
-            h_copy(0, 0, c)
+        h_tile(0, 0)
         round_w1(1, 0, "V")
         quantise_w1(1, 0)
         pick(0, 0, 0, HALF, whole=G)

@@ -93,18 +93,23 @@ def tile_list_premise_selection_kernel(tc, tab_words, tab_scales, offs, w1, offs
         v0 = sbuf([P, S], U32, "v0", "slot_v0")
         nc.vector.tensor_copy(v0[:], table0[:].bitcast(U32).indirect(idx[:]))
 
-        warm = psum.tile([P, COLS], F32, name="warm", tag="bank7")
-        for k in range(WARM):
-            nc.tensor.matmul_mx(
-                out=warm[:], lhsT=v0[:, 0:P].bitcast(FP8X4), lhsT_scale=v_sc[0][:, 0:P],
-                rhs=v0[:, 0:COLS].bitcast(FP8X4), rhs_scale=v_sc[0][:, 0:COLS], start=True, stop=True)
-
         def quantise(bf, width, name):
             lead = (48, 128) if name.startswith("w1") else (0, 64)
             codes = sbuf([P, width + lead[0]], U32, f"{name}_codes", f"slot_{name}")[:, lead[0]:]
             scales = sbuf([P, width + lead[1]], U8, f"{name}_scales")[:, lead[1]:]
             nc.vector.quantize_mx(out=codes[:].bitcast(FP8X4), scales=scales[:], in_=bf[:])
             return codes, scales
+
+        warm_bf = sbuf([P, PASS], BF16, "warm_bf")
+        nc.scalar.activation(
+            out=warm_bf[:].rearrange("p (t m j) -> p m j t", t=2, j=PACK),
+            in_=w1_raw[0, 0, 0].rearrange("p (j m t) -> p m j t", j=PACK, t=PACK)[:, :, :, 0:2], func=ACT.Copy)
+        warm_codes, warm_scales = quantise(warm_bf, P, "w1_warm")
+        warm = psum.tile([P, COLS], F32, name="warm", tag="bank7")
+        for k in range(WARM):
+            nc.tensor.matmul_mx(
+                out=warm[:], lhsT=warm_codes.bitcast(FP8X4), lhsT_scale=warm_scales,
+                rhs=v0[:, 0:COLS].bitcast(FP8X4), rhs_scale=v_sc[0][:, 0:COLS], start=True, stop=True)
 
         w1_q = {}
         w1_bf = {}
@@ -244,7 +249,7 @@ def tile_list_premise_selection_kernel(tc, tab_words, tab_scales, offs, w1, offs
         round_w1(0, 1, "S", 0, 2, "slot_h", 1, 3, 4)
         quantise_w1(0, 1, 0, 2)
         gather_v1(3, 1, "slot_h")
-        w2_wd = sbuf([P, 2, 2 * N], U8, "w2_wd", "slot_t")
+        w2_wd = sbuf([P, 192 + 4 * N], U8, "w2_wd", "slot_t")[:, 192:].rearrange("p (a c) -> p a c", a=2)
         nc.sync.dma_start(out=w2_wd[:].bitcast(I32), in_=w2_words.rearrange("a p c -> p a c").bitcast(I32))
         round_w1(0, 1, "S", 2, 2, "bf", 4, 3, 4)
         round_w1(0, 1, "S", 2, 2, "bf", 4, 2, 4)

@@ -23,7 +23,6 @@ COLS = 512
 HALF = G // 2
 QUARTER = G // 4
 EARLY = [(0, 0), (0, 1), (0, 2), (0, 3), (1, 0)]
-WARM = 4
 
 
 def tile_list_premise_selection_kernel(tc, tab_words, tab_scales, offs, w1, offs2, wgt, w2_words, w2_scales, out):
@@ -99,17 +98,6 @@ def tile_list_premise_selection_kernel(tc, tab_words, tab_scales, offs, w1, offs
             scales = sbuf([P, width + lead[1]], U8, f"{name}_scales")[:, lead[1]:]
             nc.vector.quantize_mx(out=codes[:].bitcast(FP8X4), scales=scales[:], in_=bf[:])
             return codes, scales
-
-        warm_bf = sbuf([P, PASS], BF16, "warm_bf")
-        nc.scalar.activation(
-            out=warm_bf[:].rearrange("p (t m j) -> p m j t", t=2, j=PACK),
-            in_=w1_raw[0, 0, 0].rearrange("p (j m t) -> p m j t", j=PACK, t=PACK)[:, :, :, 0:2], func=ACT.Copy)
-        warm_codes, warm_scales = quantise(warm_bf, P, "w1_warm")
-        warm = psum.tile([P, COLS], F32, name="warm", tag="bank7")
-        for k in range(WARM):
-            nc.tensor.matmul_mx(
-                out=warm[:], lhsT=warm_codes.bitcast(FP8X4), lhsT_scale=warm_scales,
-                rhs=v0[:, 0:COLS].bitcast(FP8X4), rhs_scale=v_sc[0][:, 0:COLS], start=True, stop=True)
 
         w1_q = {}
         w1_bf = {}

@@ -182,8 +182,9 @@ def tile_list_premise_selection_kernel(tc, tab_words, tab_scales, offs, w1, offs
         def round_z(b, m0, width, engine, slot="bf", bufs=4):
             base = max(m for bb, m in x_sb if bb == b and m <= m0)
             z_bf[b, m0] = sbuf([P, PACK * width], BF16, f"z_bf{b}_{m0}", slot, bufs)
-            dst = z_bf[b, m0][:].rearrange("p (c i t) -> p c t i", i=4, t=PACK)
-            src = x_sb[b, base][:, :, m0 - base:m0 - base + width].rearrange("p t (c i) -> p c t i", i=4)
+            run = 4 if engine == "V" else 2
+            dst = z_bf[b, m0][:].rearrange("p (c i t) -> p c t i", i=run, t=PACK)
+            src = x_sb[b, base][:, :, m0 - base:m0 - base + width].rearrange("p t (c i) -> p c t i", i=run)
             if engine == "V":
                 nc.vector.tensor_scalar(dst, src, 0.0, None, ALU.max)
             else:

@@ -156,7 +156,7 @@ def tile_list_premise_selection_kernel(tc, tab_words, tab_scales, offs, w1, offs
             if engine == "V":
                 nc.vector.tensor_copy(out=dst, in_=banks[b, t, c][:])
             else:
-                nc.scalar.activation(out=dst, in_=banks[b, t, c][:], func=ACT.Copy)
+                nc.scalar.copy(out=dst, in_=banks[b, t, c][:])
 
         def h_tile(b, t):
             for c in range(S // COLS):
@@ -215,7 +215,7 @@ def tile_list_premise_selection_kernel(tc, tab_words, tab_scales, offs, w1, offs
                 if engines[nt] == "V":
                     nc.vector.tensor_copy(out=res[:, nt, :], in_=acc[nt][:, 0:width])
                 else:
-                    nc.scalar.activation(out=res[:, nt, :], in_=acc[nt][:, 0:width], func=ACT.Copy)
+                    nc.scalar.copy(out=res[:, nt, :], in_=acc[nt][:, 0:width])
                 if width > P:
                     nc.sync.dma_start(out=rows[:, nt, :], in_=res[:, nt, :])
             if width == P:

from contextlib import ExitStack

import concourse.mybir as mybir

K, T, S, H, G, N = 1024, 4096, 2048, 1024, 1024, 384
FLOPS = 2 * K * H * S + 2 * H * N * G

F32 = mybir.dt.float32
BF16 = mybir.dt.bfloat16
I32 = mybir.dt.int32
U32 = mybir.dt.uint32
U16 = mybir.dt.uint16
U8 = mybir.dt.uint8
FP8X4 = mybir.dt.float8_e4m3fn_x4
FP4X4 = mybir.dt.float4_e2m1fn_x4
ALU = mybir.AluOpType
ACT = mybir.ActivationFunctionType

P = 128
PACK = 4
PASS = P * PACK
COLS = 512
HALF = G // 2
QUARTER = G // 4
EARLY = [(0, 0), (0, 1), (0, 2), (0, 3), (1, 0)]


def tile_list_premise_selection_kernel(tc, tab_words, tab_scales, offs, w1, offs2, wgt, w2_words, w2_scales, out):
    nc = tc.nc
    with ExitStack() as ctx:
        lists = ctx.enter_context(tc.tile_pool(name="lists", bufs=1))
        keep = ctx.enter_context(tc.tile_pool(name="keep", bufs=1))
        psum = ctx.enter_context(tc.psum_pool(name="psum", bufs=1))

        def sbuf(shape, dtype, name, slot=None, bufs=1):
            return keep.tile(shape, dtype, name=name, tag=slot or name, bufs=bufs, align_bytes=256)

        opened = []

        def bank():
            opened.append(psum.tile([P, COLS], F32, name="bank", tag=f"bank{len(opened) % 8}"))
            return opened[-1]

        idx = lists.tile([P, S // 16], U16, name="idx")
        idx2 = lists.tile([P, G // 16], U16, name="idx2")

        table_sc = sbuf([P, T], U8, "table_sc", "slot_a")
        table0 = sbuf([P, T], I32, "table0", "slot_b")
        table1 = sbuf([P, T], I32, "table1", "slot_t")
        picked_sc = sbuf([P, S], U8, "picked_sc", "slot_c")
        v_sc = [sbuf([P, S + 64], U8, f"v_sc{a}")[:, 64:] for a in range(2)]
        w1_raw = {}

        nc.vector.memset(table_sc[32:64, :].bitcast(I32), 0)
        nc.vector.memset(table_sc[64:P, :].bitcast(I32), 0)
        for a in range(2):
            nc.vector.memset(v_sc[a][:].bitcast(I32), 0)

        def load_w1(pieces, slot=None):
            total = sum(PASS // parts for b, a, part, parts in pieces)
            tile = sbuf([P, PACK * total], F32, "w1_raw%d%d%d" % pieces[0][:3], slot)
            at = 0
            for b, a, part, parts in pieces:
                width = PASS // parts
                w1_raw[b, a, part] = tile[:, at:at + PACK * width]
                at = at + PACK * width
                c0 = b * PASS + part * width
                nc.sync.dma_start(out=w1_raw[b, a, part].rearrange("p (j c) -> p j c", j=PACK),
                                  in_=w1[a * PASS:(a + 1) * PASS, c0:c0 + width].rearrange("(p j) c -> p j c", j=PACK))

        def load_table(tile, a):
            nc.sync.dma_start(out=tile[:], in_=tab_words[a].rearrange("p t i -> p (t i)").bitcast(I32))

        def place_scales(a):
            for q in (0, 2, 1, 3):
                nc.sync.dma_start(out=v_sc[a][32 * q + 4 * a:32 * q + 4 * a + 4, :].bitcast(I32),
                                  in_=picked_sc[16 * a + 4 * q:16 * a + 4 * q + 4, :].bitcast(I32))

        nc.sync.dma_start(idx[:], offs)
        nc.sync.dma_start(out=table_sc[0:32, :].bitcast(I32),
                          in_=tab_scales.rearrange("a q t -> (a q) t").bitcast(I32))
        load_table(table0, 0)
        load_w1([(0, 0, 0, 2)])
        load_table(table1, 1)
        nc.sync.dma_start(idx2[:], offs2)

        nc.vector.tensor_copy(picked_sc[:], table_sc[:].indirect(idx[:]))
        place_scales(0)
        load_w1([(0, 0, 1, 2), (0, 1, 0, 2), (0, 1, 2, 4), (0, 1, 3, 4)], "slot_a")
        place_scales(1)

        v0 = sbuf([P, S], U32, "v0", "slot_v0")
        nc.vector.tensor_copy(v0[:], table0[:].bitcast(U32).indirect(idx[:]))

        def quantise(bf, width, name):
            lead = (48, 128) if name.startswith("w1") else (0, 64)
            codes = sbuf([P, width + lead[0]], U32, f"{name}_codes", f"slot_{name}")[:, lead[0]:]
            scales = sbuf([P, width + lead[1]], U8, f"{name}_scales")[:, lead[1]:]
            nc.vector.quantize_mx(out=codes[:].bitcast(FP8X4), scales=scales[:], in_=bf[:])
            return codes, scales

        w1_q = {}
        w1_bf = {}

        def round_w1(b, a, engine, t0=0, n=PACK, slot="bf", bufs=4, part=0, parts=1):
            if (b, a, t0) not in w1_bf:
                w1_bf[b, a, t0] = sbuf([P, n * PASS], BF16, f"w1_bf{b}{a}{t0}", slot, bufs)
            share = slice(part * P // parts, (part + 1) * P // parts)
            dst = w1_bf[b, a, t0][:].rearrange("p (t m j) -> p m j t", t=n, j=PACK)[:, share]
            src = w1_raw[b, a, part].rearrange("p (j m t) -> p m j t", j=PACK, t=PACK)[:, :, :, t0:t0 + n]
            if engine == "V":
                nc.vector.tensor_copy(out=dst, in_=src)
            else:
                nc.scalar.activation(out=dst, in_=src, func=ACT.Copy)

        def quantise_w1(b, a, t0=0, n=PACK):
            codes, scales = quantise(w1_bf[b, a, t0], n * P, f"w1_{b}{a}{t0}")
            for t in range(n):
                w1_q[b, a, t0 + t] = codes[:, t * P:(t + 1) * P], scales[:, t * P:(t + 1) * P]

        after_table0 = sbuf([P, 2 * PACK * PASS + G], F32, "after_table0", "slot_b")
        wgt_sb = after_table0[:, 2 * PACK * PASS:]
        for a in range(2):
            w1_raw[1, a, 0] = after_table0[:, a * PACK * PASS:(a + 1) * PACK * PASS]
            nc.sync.dma_start(out=w1_raw[1, a, 0].rearrange("p (j c) -> p j c", j=PACK),
                              in_=w1[a * PASS:(a + 1) * PASS, PASS:].rearrange("(p j) c -> p j c", j=PACK))
            nc.sync.dma_start(out=wgt_sb[:, a * HALF:(a + 1) * HALF], in_=wgt[:, a * HALF:(a + 1) * HALF])

        v1 = {}
        h_sb = {}
        banks = {}

        def gather_v1(c0, n, slot=None):
            part = sbuf([P, n * COLS], U32, f"v1_{c0}", slot)
            nc.vector.tensor_copy(part[:], table1[:].bitcast(U32).indirect(idx[:, c0 * 32:(c0 + n) * 32]))
            for c in range(n):
                v1[c0 + c] = part[:, c * COLS:(c + 1) * COLS]

        def h_pass(b, t, c, a):
            first = (b, t, c) not in banks
            if first:
                banks[b, t, c] = bank()
            cols = slice(c * COLS, (c + 1) * COLS)
            codes, scales = w1_q[b, a, t]
            moving = v0[:, cols] if a == 0 else v1[c]
            nc.tensor.matmul_mx(
                out=banks[b, t, c][:],
                lhsT=codes.bitcast(FP8X4), lhsT_scale=scales,
                rhs=moving.bitcast(FP8X4), rhs_scale=v_sc[a][4 * a:P, cols],
                start=first, stop=not first)

        def h_copy(b, t, c, engine="S"):
            if (b, t) not in h_sb:
                h_sb[b, t] = sbuf([P, S], F32, f"h{b}{t}", f"h{(PACK * b + t) % 6}")
            dst = h_sb[b, t][:, c * COLS:(c + 1) * COLS]
            if engine == "V":
                nc.vector.tensor_copy(out=dst, in_=banks[b, t, c][:])
            else:
                nc.scalar.copy(out=dst, in_=banks[b, t, c][:])

        def h_tile(b, t):
            for c in range(S // COLS):
                h_pass(b, t, c, 1)
                if b == 1 or (t, c) not in EARLY:
                    h_pass(b, t, c, 0)
                h_copy(b, t, c)

        x_sb = {}

        def pick(b, t, m0, width, slot=None, base=None, whole=None):
            base = m0 if base is None else base
            if (b, base) not in x_sb:
                x_sb[b, base] = sbuf([P, PACK, whole or width], F32, f"x{b}_{base}", slot)
            nc.vector.tensor_tensor(
                x_sb[b, base][:, t, m0 - base:m0 - base + width],
                h_sb[b, t][:].indirect(idx2[:, m0 // 16:(m0 + width) // 16]),
                wgt_sb[:, m0:m0 + width], ALU.mult)

        z_q = {}
        z_bf = {}

        def round_z(b, m0, width, engine, slot="bf", bufs=4):
            base = max(m for bb, m in x_sb if bb == b and m <= m0)
            z_bf[b, m0] = sbuf([P, PACK * width], BF16, f"z_bf{b}_{m0}", slot, bufs)
            run = 4 if engine == "V" else 2
            dst = z_bf[b, m0][:].rearrange("p (c i t) -> p c t i", i=run, t=PACK)
            src = x_sb[b, base][:, :, m0 - base:m0 - base + width].rearrange("p t (c i) -> p c t i", i=run)
            if engine == "V":
                nc.vector.tensor_scalar(dst, src, 0.0, None, ALU.max)
            else:
                nc.scalar.activation(out=dst, in_=src, func=ACT.Relu)

        def quantise_z(b, m0, width):
            z_q[b, m0] = quantise(z_bf[b, m0], width, f"z{b}_{m0}")

        def scores(m0, width, engines):
            step = COLS if width == COLS else P
            acc = [bank() for nt in range(N // P)]
            for b in range(2):
                base = m0 if (b, m0) in z_q else m0 // HALF * HALF
                codes, scales = z_q[b, base]
                for nt in range(N // P):
                    for c0 in range(0, width, step):
                        cols = slice(m0 - base + c0, m0 - base + c0 + step)
                        nc.tensor.matmul_mx(
                            out=acc[nt][:, c0:c0 + step],
                            lhsT=w2_wd[:, b, 2 * P * nt:2 * P * (nt + 1)].bitcast(FP4X4),
                            lhsT_scale=w2_sc[:, b * N + nt * P:b * N + (nt + 1) * P],
                            rhs=codes[:, cols].bitcast(FP8X4),
                            rhs_scale=scales[:, cols],
                            start=(b == 0 and c0 == 0), stop=(b == 1 and c0 + step == width))
            res = sbuf([P, N // P, width], F32, f"res{m0}")
            rows = out[:, m0:m0 + width].rearrange("(nt p) m -> p nt m", p=P)
            for nt in range(N // P):
                if engines[nt] == "V":
                    nc.vector.tensor_copy(out=res[:, nt, :], in_=acc[nt][:, 0:width])
                else:
                    nc.scalar.copy(out=res[:, nt, :], in_=acc[nt][:, 0:width])
                if width > P:
                    nc.sync.dma_start(out=rows[:, nt, :], in_=res[:, nt, :])
            if width == P:
                nc.sync.dma_start(out=rows, in_=res[:])

        late_bf = sbuf([P, 2, 2 * PASS], BF16, "late_bf")
        for a in range(2):
            w1_bf[0, a, 2] = late_bf[:, a, :]
        gather_v1(0, 2)
        round_w1(0, 0, "S", 0, 2, "slot_g", 1, 0, 2)
        round_w1(0, 0, "S", 2, 2, "bf", 4, 0, 2)
        round_w1(0, 0, "S", 0, 2, "slot_g", 1, 1, 2)
        quantise_w1(0, 0, 0, 2)
        for t, c in EARLY:
            h_pass(0, t, c, 0)
        gather_v1(2, 1, "slot_g")
        round_w1(0, 0, "S", 2, 2, "bf", 4, 1, 2)
        round_w1(0, 1, "S", 0, 2, "slot_h", 1, 0, 2)
        round_w1(0, 1, "S", 0, 2, "slot_h", 1, 2, 4)
        round_w1(0, 1, "S", 0, 2, "slot_h", 1, 3, 4)
        quantise_w1(0, 1, 0, 2)
        gather_v1(3, 1, "slot_h")
        w2_wd = sbuf([P, 192 + 4 * N], U8, "w2_wd", "slot_t")[:, 192:].rearrange("p (a c) -> p a c", a=2)
        nc.sync.dma_start(out=w2_wd[:].bitcast(I32), in_=w2_words.rearrange("a p c -> p a c").bitcast(I32))
        round_w1(0, 1, "S", 2, 2, "bf", 4, 3, 4)
        round_w1(0, 1, "S", 2, 2, "bf", 4, 2, 4)
        round_w1(0, 1, "S", 2, 2, "bf", 4, 0, 2)
        late_codes = sbuf([P, PASS + 48], U32, "late_codes")[:, 48:]
        late_scales = sbuf([P, PASS + 128], U8, "late_scales")[:, 128:]
        nc.vector.quantize_mx(out=late_codes[:].bitcast(FP8X4), scales=late_scales[:],
                              in_=late_bf[:].rearrange("p a c -> p (a c)"))
        for a in range(2):
            for t in range(2, PACK):
                cols = slice((2 * a + t - 2) * P, (2 * a + t - 1) * P)
                w1_q[0, a, t] = late_codes[:, cols], late_scales[:, cols]
        w2_sc = sbuf([P, 2 * N], U8, "w2_sc", "slot_a")
        nc.gpsimd.memset(w2_sc[:].bitcast(I32), 0)
        for q in range(4):
            nc.sync.dma_start(
                out=w2_sc[32 * q:32 * q + 4, :].rearrange("r (a n) -> r a n", a=2).bitcast(I32),
                in_=w2_scales[:, 4 * q:4 * q + 4, :].rearrange("a r n -> r a n").bitcast(I32))
        h_tile(0, 0)
        round_w1(1, 0, "V")
        quantise_w1(1, 0)
        pick(0, 0, 0, HALF, whole=G)
        round_w1(1, 1, "V")
        pick(0, 0, HALF, HALF, base=0)
        quantise_w1(1, 1)
        for t in range(1, PACK):
            h_tile(0, t)
            pick(0, t, 0, G)
        for t in range(PACK):
            h_tile(1, t)
            pick(1, t, 0, G - QUARTER)
        round_z(0, 0, HALF, "S", slot="slot_v0", bufs=1)
        quantise_z(0, 0, HALF)
        round_z(0, HALF, HALF, "S", slot="slot_w1_100", bufs=1)
        quantise_z(0, HALF, HALF)
        round_z(1, 0, HALF, "S", slot="slot_f", bufs=1)
        quantise_z(1, 0, HALF)
        round_z(1, HALF, QUARTER, "S")
        quantise_z(1, HALF, QUARTER)
        for t in range(PACK):
            pick(1, t, G - 2 * P, P, "slot_w1_100")
        round_z(1, G - 2 * P, P, "S")
        quantise_z(1, G - 2 * P, P)
        scores(0, HALF, "SSS")
        for t in range(PACK):
            pick(1, t, G - P, P, "slot_f")
        scores(HALF, QUARTER, "SSS")
        scores(G - 2 * P, P, "VVV")
        round_z(1, G - P, P, "V")
        quantise_z(1, G - P, P)
        scores(G - P, P, "VVS")
